import numpy as np
import ml_dtypes


def mxq(x, axis, fmt="e4m3"):
    dtype, down = {"e4m3": (ml_dtypes.float8_e4m3fn, 7), "e5m2": (ml_dtypes.float8_e5m2, 14)}[fmt]
    v = np.moveaxis(np.asarray(x, np.float32).astype(ml_dtypes.bfloat16).astype(np.float64), axis, -1)
    blocks = v.reshape(v.shape[:-1] + (-1, 32))
    amax = np.abs(blocks).max(-1, keepdims=True)
    byte = np.maximum(np.where(amax > 0, np.frexp(amax)[1] - 1 + 127, 0) - down, 1)
    scale = np.exp2(byte - 127.0)
    codes = (blocks / scale).astype(np.float32).astype(dtype).astype(np.float64)
    return np.moveaxis((codes * scale).reshape(v.shape), -1, axis)


WIDE = False


def mx_kscale(k):
    if not WIDE:
        return np.ones(k)
    levels = np.array([10, -10, 5, -5, 0])
    if k % 512:
        return np.exp2(np.random.permutation(np.resize(levels, k // 32))).repeat(32)
    a = np.empty((k // 512, 16))
    for p in range(k // 512):
        a[p, :8] = np.random.permutation(np.resize(levels, 8))
        for g in range(8):
            far = levels[np.abs(levels - a[p, g]) >= 10]
            a[p, g + 8] = far[np.random.randint(len(far))]
    return np.exp2(a.ravel()).repeat(32)


def f64(x):
    return np.asarray(x).astype(np.float64)


def striped(idx):
    return np.tile(np.asarray(idx).reshape(-1, 16).T, (8, 1)).astype(np.uint16)


def unstriped(offs):
    return offs[:16].T.reshape(-1).astype(np.int64)

def bf(x):
    return np.asarray(x, np.float32).astype(ml_dtypes.bfloat16)


def planes(Y):
    r, m = Y.shape
    b = f64(bf(Y)).reshape(r // 32, 32, m)
    amax = np.abs(b).max(1)
    byte = np.clip(np.where(amax > 0, np.frexp(amax)[1] - 1 + 127 - 7, 1), 1, 254)
    codes = (b * np.exp2(127.0 - byte)[:, None, :]).reshape(r, m).astype(np.float32).astype(ml_dtypes.float8_e4m3fn).view(np.uint8)
    words = codes.reshape(r // 512, 128, 4, m).transpose(0, 1, 3, 2)
    return np.ascontiguousarray(words), np.ascontiguousarray(byte.astype(np.uint8).reshape(r // 512, 16, m))


B, N, T, D, NQ = 1, 512, 2048, 512, 512


def setup_inputs():
    n = np.random.standard_normal
    idx = np.random.permutation(T)[:B * N]
    s = mx_kscale(D)[:, None]
    return {
        "qT": (n((B, D, NQ)) * s * (1.00 / np.sqrt(D))).astype(np.float32),
        "kT": (n((D, T)) / s).astype(np.float32),
        "ls": (np.random.uniform(7.8, 8.4, (B, 1, NQ))).astype(np.float32),
        "offs": striped(idx),
    }


def reference(qT, kT, ls, offs):
    idx = unstriped(offs)
    pick = lambda x, which: x[:, which].reshape(x.shape[0], B, -1).transpose(1, 0, 2)
    kg = mxq(pick(f64(kT), idx), 1, "e4m3")
    qq = mxq(f64(qT), 1, "e4m3")
    a = kg.transpose(0, 2, 1) @ qq
    y = np.exp(a - f64(ls))
    Y = y[0]
    words, scales = planes(Y)
    return Y, words, scales

@@ -1,0 +1,146 @@
+from contextlib import ExitStack
+
+import concourse.mybir as mybir
+from concourse.masks import make_identity
+
+D, T, N, NQ = 512, 2048, 512, 512
+FLOPS = 2 * N * NQ * D
+
+F32 = mybir.dt.float32
+BF16 = mybir.dt.bfloat16
+I32 = mybir.dt.int32
+U32 = mybir.dt.uint32
+U16 = mybir.dt.uint16
+U8 = mybir.dt.uint8
+FP8X4 = mybir.dt.float8_e4m3fn_x4
+EXP = mybir.ActivationFunctionType.Exp
+SUB = mybir.AluOpType.subtract
+
+P = 128
+PACK = 4
+QC = 128
+CHUNKS = NQ // QC
+Q_LOADS = (128, 128, 256)
+PIECES = (128, 128, 128, 64, 64)
+
+
+def weave(engine_copy, dst, src):
+    engine_copy(
+        out=dst.rearrange("p (c i) t -> p c t i", i=PACK),
+        in_=src.rearrange("p t (c i) -> p c t i", i=PACK),
+    )
+
+
+def tile_attend_plw_softf_f_topk_kernel(tc, qT, kT, ls, offs, out_0, out_1, out_2):
+    nc = tc.nc
+    with ExitStack() as ctx:
+        keep = ctx.enter_context(tc.tile_pool(name="keep", bufs=1))
+        psum = ctx.enter_context(tc.psum_pool(name="psum", bufs=1))
+
+        offsets = keep.tile([P, N // 16], U16, name="offsets")
+        ls_col = keep.tile([P, PACK], F32, name="ls_col")
+        planes = [keep.tile([P, T], F32, name=f"plane{t}") for t in range(PACK)]
+        q_raw = [keep.tile([P, PACK, w], F32, name=f"q_raw{h}") for h, w in enumerate(Q_LOADS)]
+
+        k_rows = kT.rearrange("(p t) n -> t p n", t=PACK)
+        q_rows = qT[0].rearrange("(p t) n -> p t n", t=PACK)
+        nc.sync.dma_start(out=planes[0][:], in_=k_rows[0])
+        nc.sync.dma_start(offsets[:], offs)
+        nc.sync.dma_start(out=ls_col[:], in_=ls[0, 0].rearrange("(p c) -> p c", c=PACK))
+        for t in range(1, PACK):
+            nc.sync.dma_start(out=planes[t][:], in_=k_rows[t])
+        q_src = []
+        for h, w in enumerate(Q_LOADS):
+            first = sum(Q_LOADS[:h])
+            nc.sync.dma_start(out=q_raw[h][:], in_=q_rows[:, :, first : first + w])
+            q_src.extend(q_raw[h][:, :, lo : lo + QC] for lo in range(0, w, QC))
+
+        ident = keep.tile([P, P], F32, name="ident")
+        make_identity(nc, ident[:])
+        warm = keep.tile([P, 1], F32, name="warm")
+        nc.scalar.activation(out=warm[:], in_=ident[:, 0:1], func=EXP)
+
+        ls_ps = psum.tile([P, PACK, P], F32, name="ls_ps")
+        for c in range(PACK):
+            nc.tensor.transpose(ls_ps[:, c, :], ls_col[:, c : c + 1].to_broadcast([P, P]), ident[:])
+        ls_all = keep.tile([P, NQ], F32, name="ls_all")
+        nc.scalar.copy(
+            out=ls_all[:].rearrange("p (n c) -> p n c", c=PACK),
+            in_=ls_ps[:].rearrange("p c n -> p n c"),
+        )
+
+        k_bf = keep.tile([P, N * PACK], BF16, name="k_bf", align_bytes=64)
+        k_dealt = k_bf[:].rearrange("p (r s t) -> p s r t", r=PACK, t=PACK)
+        for t in range(PACK):
+            nc.vector.tensor_copy(out=k_dealt[:, :, :, t], in_=planes[t][:].indirect(offsets[:]))
+
+        q_bf = [keep.tile([P, QC, PACK], BF16, name=f"q_bf{c}", align_bytes=64) for c in range(CHUNKS)]
+        q_codes = [keep.tile([P, QC], U32, name=f"q_codes{c}", align_bytes=64) for c in range(CHUNKS)]
+        q_scales = [keep.tile([P, QC], U8, name=f"q_scales{c}", align_bytes=64) for c in range(CHUNKS)]
+        k_codes = [keep.tile([P, P], U32, name=f"k_codes{r}", align_bytes=64) for r in range(PACK)]
+        k_scales = [keep.tile([P, P], U8, name=f"k_scales{r}", align_bytes=64) for r in range(PACK)]
+
+        def quantize(codes, scales, values):
+            nc.vector.quantize_mx(out=codes.bitcast(FP8X4), scales=scales, in_=values)
+
+        def quantize_q(c):
+            quantize(q_codes[c][:], q_scales[c][:], q_bf[c][:].rearrange("p c t -> p (c t)"))
+
+        for c in range(CHUNKS):
+            weave(nc.scalar.copy, q_bf[c][:], q_src[c])
+        quantize_q(0)
+        for r in range(PACK):
+            quantize(k_codes[r][:], k_scales[r][:], k_bf[:, r * P * PACK : (r + 1) * P * PACK])
+        for c in range(1, CHUNKS):
+            quantize_q(c)
+
+        y_rows = out_0.rearrange("(p r) q -> p r q", r=PACK)
+        y_words_hbm = out_1[0].rearrange("p q t -> p (q t)").bitcast(I32)
+        y_scales_hbm = out_2[0].bitcast(I32)
+        y_scales = keep.tile([P, NQ], U8, name="y_scales", align_bytes=64)
+
+        scores = []
+        for c in range(CHUNKS):
+            scores.append(psum.tile([P, PACK, QC], F32, name=f"scores{c}"))
+            for r in range(PACK):
+                nc.tensor.matmul_mx(
+                    out=scores[c][:, r, :],
+                    lhsT=k_codes[r][:].bitcast(FP8X4),
+                    lhsT_scale=k_scales[r][:],
+                    rhs=q_codes[c][:].bitcast(FP8X4),
+                    rhs_scale=q_scales[c][:],
+                    start=True,
+                    stop=True,
+                )
+
+        y = []
+        for j, w in enumerate(PIECES):
+            first = sum(PIECES[:j])
+            cols = slice(first, first + w)
+            c, lo = divmod(first, QC)
+            shifted = keep.tile([P, PACK, w], F32, name=f"shifted{j}")
+            nc.vector.tensor_tensor(
+                out=shifted[:],
+                in0=scores[c][:, :, lo : lo + w],
+                in1=ls_all[:, cols].unsqueeze(1).to_broadcast([P, PACK, w]),
+                op=SUB,
+            )
+            y.append(keep.tile([P, PACK, w], F32, name=f"y{j}"))
+            nc.scalar.activation(out=y[j][:], in_=shifted[:], func=EXP)
+            nc.sync.dma_start(out=y_rows[:, :, cols], in_=y[j][:])
+
+        for j, w in enumerate(PIECES):
+            first = sum(PIECES[:j])
+            cols = slice(first, first + w)
+            y_bf = keep.tile([P, w, PACK], BF16, name=f"y_bf{j}", align_bytes=64)
+            weave(nc.vector.tensor_copy, y_bf[:], y[j][:])
+            y_codes = keep.tile([P, w], U32, name=f"y_codes{j}", align_bytes=64)
+            quantize(y_codes[:], y_scales[:, cols], y_bf[:].rearrange("p c t -> p (c t)"))
+            nc.sync.dma_start(out=y_words_hbm[:, cols], in_=y_codes[:].bitcast(I32))
+
+        for quad in range(4):
+            queue = nc.scalar if quad % 2 else nc.sync
+            queue.dma_start(
+                out=y_scales_hbm[4 * quad : 4 * quad + 4, :],
+                in_=y_scales[32 * quad : 32 * quad + 4, :].bitcast(I32),
+            )

@@ -20,8 +20,10 @@ P = 128
 PACK = 4
 QC = 128
 CHUNKS = NQ // QC
-Q_LOADS = (128, 128, 256)
-PIECES = (128, 128, 128, 64, 64)
+Q_LOADS = (128, 128, 128, 128)
+PIECES = (128, 128, 128, 128)
+WORD_STORES = (256, 512)
+SCALAR_WEAVES = (3,)
 
 
 def weave(engine_copy, dst, src):
@@ -46,7 +48,7 @@ def tile_attend_plw_softf_f_topk_kernel(tc, qT, kT, ls, offs, out_0, out_1, out_
         q_rows = qT[0].rearrange("(p t) n -> p t n", t=PACK)
         nc.sync.dma_start(out=planes[0][:], in_=k_rows[0])
         nc.sync.dma_start(offsets[:], offs)
-        nc.sync.dma_start(out=ls_col[:], in_=ls[0, 0].rearrange("(p c) -> p c", c=PACK))
+        nc.scalar.dma_start(out=ls_col[:], in_=ls[0, 0].rearrange("(p c) -> p c", c=PACK))
         for t in range(1, PACK):
             nc.sync.dma_start(out=planes[t][:], in_=k_rows[t])
         q_src = []
@@ -74,10 +76,9 @@ def tile_attend_plw_softf_f_topk_kernel(tc, qT, kT, ls, offs, out_0, out_1, out_
         for t in range(PACK):
             nc.vector.tensor_copy(out=k_dealt[:, :, :, t], in_=planes[t][:].indirect(offsets[:]))
 
-        q_bf = [keep.tile([P, QC, PACK], BF16, name=f"q_bf{c}", align_bytes=64) for c in range(CHUNKS)]
+        q_bf = [keep.tile([P, QC, PACK], BF16, name=f"q_bf{c}", tag=f"stage{c}", align_bytes=64) for c in range(CHUNKS)]
         q_codes = [keep.tile([P, QC], U32, name=f"q_codes{c}", align_bytes=64) for c in range(CHUNKS)]
         q_scales = [keep.tile([P, QC], U8, name=f"q_scales{c}", align_bytes=64) for c in range(CHUNKS)]
-        k_codes = [keep.tile([P, P], U32, name=f"k_codes{r}", align_bytes=64) for r in range(PACK)]
         k_scales = [keep.tile([P, P], U8, name=f"k_scales{r}", align_bytes=64) for r in range(PACK)]
 
         def quantize(codes, scales, values):
@@ -89,8 +90,10 @@ def tile_attend_plw_softf_f_topk_kernel(tc, qT, kT, ls, offs, out_0, out_1, out_
         for c in range(CHUNKS):
             weave(nc.scalar.copy, q_bf[c][:], q_src[c])
         quantize_q(0)
+        k_words = keep.tile([P, N], U32, name="k_words", tag="stage0", align_bytes=64)
+        k_codes = [k_words[:, r * P : (r + 1) * P] for r in range(PACK)]
         for r in range(PACK):
-            quantize(k_codes[r][:], k_scales[r][:], k_bf[:, r * P * PACK : (r + 1) * P * PACK])
+            quantize(k_codes[r], k_scales[r][:], k_bf[:, r * P * PACK : (r + 1) * P * PACK])
         for c in range(1, CHUNKS):
             quantize_q(c)
 
@@ -105,7 +108,7 @@ def tile_attend_plw_softf_f_topk_kernel(tc, qT, kT, ls, offs, out_0, out_1, out_
             for r in range(PACK):
                 nc.tensor.matmul_mx(
                     out=scores[c][:, r, :],
-                    lhsT=k_codes[r][:].bitcast(FP8X4),
+                    lhsT=k_codes[r].bitcast(FP8X4),
                     lhsT_scale=k_scales[r][:],
                     rhs=q_codes[c][:].bitcast(FP8X4),
                     rhs_scale=q_scales[c][:],
@@ -118,7 +121,8 @@ def tile_attend_plw_softf_f_topk_kernel(tc, qT, kT, ls, offs, out_0, out_1, out_
             first = sum(PIECES[:j])
             cols = slice(first, first + w)
             c, lo = divmod(first, QC)
-            shifted = keep.tile([P, PACK, w], F32, name=f"shifted{j}")
+            tag = f"stage{CHUNKS - 1}" if j == 1 else f"shifted{j}"
+            shifted = keep.tile([P, PACK, w], F32, name=f"shifted{j}", tag=tag, align_bytes=64)
             nc.vector.tensor_tensor(
                 out=shifted[:],
                 in0=scores[c][:, :, lo : lo + w],
@@ -129,14 +133,18 @@ def tile_attend_plw_softf_f_topk_kernel(tc, qT, kT, ls, offs, out_0, out_1, out_
             nc.scalar.activation(out=y[j][:], in_=shifted[:], func=EXP)
             nc.sync.dma_start(out=y_rows[:, :, cols], in_=y[j][:])
 
+        y_codes = keep.tile([P, NQ], U32, name="y_codes", align_bytes=64)
+        stored = 0
         for j, w in enumerate(PIECES):
             first = sum(PIECES[:j])
             cols = slice(first, first + w)
             y_bf = keep.tile([P, w, PACK], BF16, name=f"y_bf{j}", align_bytes=64)
-            weave(nc.vector.tensor_copy, y_bf[:], y[j][:])
-            y_codes = keep.tile([P, w], U32, name=f"y_codes{j}", align_bytes=64)
-            quantize(y_codes[:], y_scales[:, cols], y_bf[:].rearrange("p c t -> p (c t)"))
-            nc.sync.dma_start(out=y_words_hbm[:, cols], in_=y_codes[:].bitcast(I32))
+            weave(nc.scalar.copy if j in SCALAR_WEAVES else nc.vector.tensor_copy, y_bf[:], y[j][:])
+            quantize(y_codes[:, cols], y_scales[:, cols], y_bf[:].rearrange("p c t -> p (c t)"))
+            if first + w in WORD_STORES:
+                done = slice(stored, first + w)
+                nc.sync.dma_start(out=y_words_hbm[:, done], in_=y_codes[:, done].bitcast(I32))
+                stored = first + w
 
         for quad in range(4):
             queue = nc.scalar if quad % 2 else nc.sync

@@ -22,6 +22,7 @@ QC = 128
 CHUNKS = NQ // QC
 Q_LOADS = (128, 128, 128, 128)
 PIECES = (128, 128, 128, 128)
+Y_STORES = (128, 128, 256)
 WORD_STORES = (256, 512)
 SCALAR_WEAVES = (3,)
 
@@ -42,7 +43,7 @@ def tile_attend_plw_softf_f_topk_kernel(tc, qT, kT, ls, offs, out_0, out_1, out_
         offsets = keep.tile([P, N // 16], U16, name="offsets")
         ls_col = keep.tile([P, PACK], F32, name="ls_col")
         planes = [keep.tile([P, T], F32, name=f"plane{t}") for t in range(PACK)]
-        q_raw = [keep.tile([P, PACK, w], F32, name=f"q_raw{h}") for h, w in enumerate(Q_LOADS)]
+        q_raw = [keep.tile([P, PACK, w], F32, name=f"q_raw{h}", tag=f"stage{h}", align_bytes=64) for h, w in enumerate(Q_LOADS)]
 
         k_rows = kT.rearrange("(p t) n -> t p n", t=PACK)
         q_rows = qT[0].rearrange("(p t) n -> p t n", t=PACK)
@@ -73,11 +74,20 @@ def tile_attend_plw_softf_f_topk_kernel(tc, qT, kT, ls, offs, out_0, out_1, out_
 
         k_bf = keep.tile([P, N * PACK], BF16, name="k_bf", align_bytes=64)
         k_dealt = k_bf[:].rearrange("p (r s t) -> p s r t", r=PACK, t=PACK)
-        for t in range(PACK):
-            nc.vector.tensor_copy(out=k_dealt[:, :, :, t], in_=planes[t][:].indirect(offsets[:]))
+        early = keep.tile([P, 2, N], BF16, name="early")
+        for t in range(2):
+            nc.vector.tensor_copy(out=early[:, t, :], in_=planes[t][:].indirect(offsets[:]))
+        nc.scalar.copy(
+            out=k_dealt[:, :, :, 0:2].rearrange("p s r t -> p s t r"),
+            in_=early[:].rearrange("p t (s r) -> p s t r", r=PACK),
+        )
+        third = keep.tile([P, N], BF16, name="third")
+        nc.vector.tensor_copy(out=third[:], in_=planes[2][:].indirect(offsets[:]))
+        nc.vector.tensor_copy(out=k_dealt[:, :, :, 2], in_=third[:].rearrange("p (s r) -> p s r", r=PACK))
+        nc.vector.tensor_copy(out=k_dealt[:, :, :, 3], in_=planes[3][:].indirect(offsets[:]))
 
-        q_bf = [keep.tile([P, QC, PACK], BF16, name=f"q_bf{c}", tag=f"stage{c}", align_bytes=64) for c in range(CHUNKS)]
-        q_codes = [keep.tile([P, QC], U32, name=f"q_codes{c}", align_bytes=64) for c in range(CHUNKS)]
+        q_bf = [keep.tile([P, QC, PACK], BF16, name=f"q_bf{c}", align_bytes=64) for c in range(CHUNKS)]
+        q_codes = [keep.tile([P, QC], U32, name=f"q_codes{c}", tag=f"q_codes{c}", align_bytes=64) for c in range(CHUNKS)]
         q_scales = [keep.tile([P, QC], U8, name=f"q_scales{c}", align_bytes=64) for c in range(CHUNKS)]
         k_scales = [keep.tile([P, P], U8, name=f"k_scales{r}", align_bytes=64) for r in range(PACK)]
 
@@ -117,6 +127,12 @@ def tile_attend_plw_softf_f_topk_kernel(tc, qT, kT, ls, offs, out_0, out_1, out_
                 )
 
         y = []
+        y_stores = {}
+        for h, w in enumerate(Y_STORES):
+            first = sum(Y_STORES[:h])
+            y_tile = keep.tile([P, PACK, w], F32, name=f"y{h}")
+            y_stores[first + w] = (y_tile, first)
+            y.extend(y_tile[:, :, lo : lo + QC] for lo in range(0, w, QC))
         for j, w in enumerate(PIECES):
             first = sum(PIECES[:j])
             cols = slice(first, first + w)
@@ -129,22 +145,20 @@ def tile_attend_plw_softf_f_topk_kernel(tc, qT, kT, ls, offs, out_0, out_1, out_
                 in1=ls_all[:, cols].unsqueeze(1).to_broadcast([P, PACK, w]),
                 op=SUB,
             )
-            y.append(keep.tile([P, PACK, w], F32, name=f"y{j}"))
-            nc.scalar.activation(out=y[j][:], in_=shifted[:], func=EXP)
-            nc.sync.dma_start(out=y_rows[:, :, cols], in_=y[j][:])
+            nc.scalar.activation(out=y[j], in_=shifted[:], func=EXP)
+            if first + w in y_stores:
+                tile, start = y_stores[first + w]
+                nc.sync.dma_start(out=y_rows[:, :, start : first + w], in_=tile[:])
 
         y_codes = keep.tile([P, NQ], U32, name="y_codes", align_bytes=64)
-        stored = 0
-        for j, w in enumerate(PIECES):
-            first = sum(PIECES[:j])
-            cols = slice(first, first + w)
-            y_bf = keep.tile([P, w, PACK], BF16, name=f"y_bf{j}", align_bytes=64)
-            weave(nc.scalar.copy if j in SCALAR_WEAVES else nc.vector.tensor_copy, y_bf[:], y[j][:])
-            quantize(y_codes[:, cols], y_scales[:, cols], y_bf[:].rearrange("p c t -> p (c t)"))
-            if first + w in WORD_STORES:
-                done = slice(stored, first + w)
-                nc.sync.dma_start(out=y_words_hbm[:, done], in_=y_codes[:, done].bitcast(I32))
-                stored = first + w
+        y_bf = keep.tile([P, NQ * PACK], BF16, name="y_bf", tag=f"q_codes{CHUNKS - 1}", align_bytes=64)
+        for c in range(CHUNKS):
+            piece = y_bf[:, c * QC * PACK : (c + 1) * QC * PACK].rearrange("p (c t) -> p c t", t=PACK)
+            weave(nc.scalar.copy if c in SCALAR_WEAVES else nc.vector.tensor_copy, piece, y[c])
+        for first in range(0, NQ, NQ // 2):
+            cols = slice(first, first + NQ // 2)
+            quantize(y_codes[:, cols], y_scales[:, cols], y_bf[:, first * PACK : (first + NQ // 2) * PACK])
+            nc.sync.dma_start(out=y_words_hbm[:, cols], in_=y_codes[:, cols].bitcast(I32))
 
         for quad in range(4):
             queue = nc.scalar if quad % 2 else nc.sync

@@ -14,21 +14,22 @@ U16 = mybir.dt.uint16
 U8 = mybir.dt.uint8
 FP8X4 = mybir.dt.float8_e4m3fn_x4
 EXP = mybir.ActivationFunctionType.Exp
+COPY = mybir.ActivationFunctionType.Copy
 SUB = mybir.AluOpType.subtract
 
 P = 128
 PACK = 4
+LIST_ROWS = 16
+QUADRANT = 32
 QC = 128
 CHUNKS = NQ // QC
-Q_LOADS = (128, 128, 128, 128)
-PIECES = (128, 128, 128, 128)
-Y_STORES = (128, 128, 256)
-WORD_STORES = (256, 512)
-SCALAR_WEAVES = (3,)
+LAST = CHUNKS - 1
+Q_LOADS = (2 * QC, QC, QC)
+HALF = NQ // 2
 
 
-def weave(engine_copy, dst, src):
-    engine_copy(
+def weave(copy, dst, src):
+    copy(
         out=dst.rearrange("p (c i) t -> p c t i", i=PACK),
         in_=src.rearrange("p t (c i) -> p c t i", i=PACK),
     )
@@ -36,15 +37,21 @@ def weave(engine_copy, dst, src):
 
 def tile_attend_plw_softf_f_topk_kernel(tc, qT, kT, ls, offs, out_0, out_1, out_2):
     nc = tc.nc
+
+    def quantize(codes, scales, values):
+        nc.vector.quantize_mx(out=codes.bitcast(FP8X4), scales=scales, in_=values)
+
     with ExitStack() as ctx:
         keep = ctx.enter_context(tc.tile_pool(name="keep", bufs=1))
         psum = ctx.enter_context(tc.psum_pool(name="psum", bufs=1))
 
-        offsets = keep.tile([P, N // 16], U16, name="offsets")
+        offsets = keep.tile([P, N // LIST_ROWS], U16, name="offsets")
         ls_col = keep.tile([P, PACK], F32, name="ls_col")
         planes = [keep.tile([P, T], F32, name=f"plane{t}") for t in range(PACK)]
-        q_raw = [keep.tile([P, PACK, w], F32, name=f"q_raw{h}", tag=f"stage{h}", align_bytes=64) for h, w in enumerate(Q_LOADS)]
-
+        q_raw = [
+            keep.tile([P, PACK, w], F32, name=f"q_raw{h}", tag=f"q_raw{h}", align_bytes=64)
+            for h, w in enumerate(Q_LOADS)
+        ]
         k_rows = kT.rearrange("(p t) n -> t p n", t=PACK)
         q_rows = qT[0].rearrange("(p t) n -> p t n", t=PACK)
         nc.sync.dma_start(out=planes[0][:], in_=k_rows[0])
@@ -52,72 +59,70 @@ def tile_attend_plw_softf_f_topk_kernel(tc, qT, kT, ls, offs, out_0, out_1, out_
         nc.scalar.dma_start(out=ls_col[:], in_=ls[0, 0].rearrange("(p c) -> p c", c=PACK))
         for t in range(1, PACK):
             nc.sync.dma_start(out=planes[t][:], in_=k_rows[t])
-        q_src = []
+        q_chunks = []
         for h, w in enumerate(Q_LOADS):
             first = sum(Q_LOADS[:h])
             nc.sync.dma_start(out=q_raw[h][:], in_=q_rows[:, :, first : first + w])
-            q_src.extend(q_raw[h][:, :, lo : lo + QC] for lo in range(0, w, QC))
+            q_chunks.extend(q_raw[h][:, :, lo : lo + QC] for lo in range(0, w, QC))
 
         ident = keep.tile([P, P], F32, name="ident")
         make_identity(nc, ident[:])
-        warm = keep.tile([P, 1], F32, name="warm")
-        nc.scalar.activation(out=warm[:], in_=ident[:, 0:1], func=EXP)
-
         ls_ps = psum.tile([P, PACK, P], F32, name="ls_ps")
         for c in range(PACK):
             nc.tensor.transpose(ls_ps[:, c, :], ls_col[:, c : c + 1].to_broadcast([P, P]), ident[:])
         ls_all = keep.tile([P, NQ], F32, name="ls_all")
-        nc.scalar.copy(
+        nc.scalar.activation(
             out=ls_all[:].rearrange("p (n c) -> p n c", c=PACK),
             in_=ls_ps[:].rearrange("p c n -> p n c"),
+            func=COPY,
         )
 
         k_bf = keep.tile([P, N * PACK], BF16, name="k_bf", align_bytes=64)
         k_dealt = k_bf[:].rearrange("p (r s t) -> p s r t", r=PACK, t=PACK)
-        early = keep.tile([P, 2, N], BF16, name="early")
+        gathered01 = keep.tile([P, 2, N], BF16, name="gathered01")
         for t in range(2):
-            nc.vector.tensor_copy(out=early[:, t, :], in_=planes[t][:].indirect(offsets[:]))
+            nc.vector.tensor_copy(out=gathered01[:, t, :], in_=planes[t][:].indirect(offsets[:]))
         nc.scalar.copy(
             out=k_dealt[:, :, :, 0:2].rearrange("p s r t -> p s t r"),
-            in_=early[:].rearrange("p t (s r) -> p s t r", r=PACK),
+            in_=gathered01[:].rearrange("p t (s r) -> p s t r", r=PACK),
         )
-        third = keep.tile([P, N], BF16, name="third")
-        nc.vector.tensor_copy(out=third[:], in_=planes[2][:].indirect(offsets[:]))
-        nc.vector.tensor_copy(out=k_dealt[:, :, :, 2], in_=third[:].rearrange("p (s r) -> p s r", r=PACK))
+        gathered2 = keep.tile([P, N], BF16, name="gathered2")
+        nc.vector.tensor_copy(out=gathered2[:], in_=planes[2][:].indirect(offsets[:]))
+        nc.vector.tensor_copy(out=k_dealt[:, :, :, 2], in_=gathered2[:].rearrange("p (s r) -> p s r", r=PACK))
         nc.vector.tensor_copy(out=k_dealt[:, :, :, 3], in_=planes[3][:].indirect(offsets[:]))
 
         q_bf = [keep.tile([P, QC, PACK], BF16, name=f"q_bf{c}", align_bytes=64) for c in range(CHUNKS)]
-        q_codes = [keep.tile([P, QC], U32, name=f"q_codes{c}", tag=f"q_codes{c}", align_bytes=64) for c in range(CHUNKS)]
+        q_codes = [
+            keep.tile([P, QC], U32, name=f"q_codes{c}", tag=f"q_codes{c}", align_bytes=64)
+            for c in range(CHUNKS)
+        ]
         q_scales = [keep.tile([P, QC], U8, name=f"q_scales{c}", align_bytes=64) for c in range(CHUNKS)]
         k_scales = [keep.tile([P, P], U8, name=f"k_scales{r}", align_bytes=64) for r in range(PACK)]
-
-        def quantize(codes, scales, values):
-            nc.vector.quantize_mx(out=codes.bitcast(FP8X4), scales=scales, in_=values)
 
         def quantize_q(c):
             quantize(q_codes[c][:], q_scales[c][:], q_bf[c][:].rearrange("p c t -> p (c t)"))
 
         for c in range(CHUNKS):
-            weave(nc.scalar.copy, q_bf[c][:], q_src[c])
+            weave(nc.scalar.copy if c else nc.vector.tensor_copy, q_bf[c][:], q_chunks[c])
         quantize_q(0)
-        k_words = keep.tile([P, N], U32, name="k_words", tag="stage0", align_bytes=64)
+        k_words = keep.tile([P, N], U32, name="k_words", tag="q_raw0", align_bytes=64)
         k_codes = [k_words[:, r * P : (r + 1) * P] for r in range(PACK)]
         for r in range(PACK):
             quantize(k_codes[r], k_scales[r][:], k_bf[:, r * P * PACK : (r + 1) * P * PACK])
         for c in range(1, CHUNKS):
             quantize_q(c)
 
-        y_rows = out_0.rearrange("(p r) q -> p r q", r=PACK)
-        y_words_hbm = out_1[0].rearrange("p q t -> p (q t)").bitcast(I32)
-        y_scales_hbm = out_2[0].bitcast(I32)
-        y_scales = keep.tile([P, NQ], U8, name="y_scales", align_bytes=64)
-
         scores = []
         for c in range(CHUNKS):
-            scores.append(psum.tile([P, PACK, QC], F32, name=f"scores{c}"))
+            tiles_a_bank = PACK if c else PACK // 2
+            banks = [
+                psum.tile([P, tiles_a_bank, QC], F32, name=f"scores{c}_{b}")
+                for b in range(PACK // tiles_a_bank)
+            ]
+            scores.append(banks)
             for r in range(PACK):
                 nc.tensor.matmul_mx(
-                    out=scores[c][:, r, :],
+                    out=banks[r // tiles_a_bank][:, r % tiles_a_bank, :],
                     lhsT=k_codes[r].bitcast(FP8X4),
                     lhsT_scale=k_scales[r][:],
                     rhs=q_codes[c][:].bitcast(FP8X4),
@@ -126,43 +131,47 @@ def tile_attend_plw_softf_f_topk_kernel(tc, qT, kT, ls, offs, out_0, out_1, out_
                     stop=True,
                 )
 
-        y = []
-        y_stores = {}
-        for h, w in enumerate(Y_STORES):
-            first = sum(Y_STORES[:h])
-            y_tile = keep.tile([P, PACK, w], F32, name=f"y{h}")
-            y_stores[first + w] = (y_tile, first)
-            y.extend(y_tile[:, :, lo : lo + QC] for lo in range(0, w, QC))
-        for j, w in enumerate(PIECES):
-            first = sum(PIECES[:j])
-            cols = slice(first, first + w)
-            c, lo = divmod(first, QC)
-            tag = f"stage{CHUNKS - 1}" if j == 1 else f"shifted{j}"
-            shifted = keep.tile([P, PACK, w], F32, name=f"shifted{j}", tag=tag, align_bytes=64)
-            nc.vector.tensor_tensor(
-                out=shifted[:],
-                in0=scores[c][:, :, lo : lo + w],
-                in1=ls_all[:, cols].unsqueeze(1).to_broadcast([P, PACK, w]),
-                op=SUB,
-            )
-            nc.scalar.activation(out=y[j], in_=shifted[:], func=EXP)
-            if first + w in y_stores:
-                tile, start = y_stores[first + w]
-                nc.sync.dma_start(out=y_rows[:, :, start : first + w], in_=tile[:])
+        y_rows = out_0.rearrange("(p r) q -> p r q", r=PACK)
+        y_halves = [keep.tile([P, PACK, HALF], F32, name=f"y{h}") for h in range(NQ // HALF)]
+        y = [half[:, :, lo : lo + QC] for half in y_halves for lo in range(0, HALF, QC)]
+        for c in range(CHUNKS):
+            tag = f"q_raw{len(Q_LOADS) - 1}" if c == 1 else f"shifted{c}"
+            shifted = keep.tile([P, PACK, QC], F32, name=f"shifted{c}", tag=tag, align_bytes=64)
+            tiles_a_bank = PACK // len(scores[c])
+            w = QC // 2 if c == LAST else QC
+            for lo in range(0, QC, w):
+                first = c * QC + lo
+                for b, bank in enumerate(scores[c]):
+                    nc.vector.tensor_tensor(
+                        out=shifted[:, b * tiles_a_bank : (b + 1) * tiles_a_bank, lo : lo + w],
+                        in0=bank[:, :, lo : lo + w],
+                        in1=ls_all[:, first : first + w].unsqueeze(1).to_broadcast([P, tiles_a_bank, w]),
+                        op=SUB,
+                    )
+                nc.scalar.activation(out=y[c][:, :, lo : lo + w], in_=shifted[:, :, lo : lo + w], func=EXP)
+            h, rest = divmod((c + 1) * QC, HALF)
+            if rest == 0:
+                nc.sync.dma_start(out=y_rows[:, :, (h - 1) * HALF : h * HALF], in_=y_halves[h - 1][:])
 
         y_codes = keep.tile([P, NQ], U32, name="y_codes", align_bytes=64)
-        y_bf = keep.tile([P, NQ * PACK], BF16, name="y_bf", tag=f"q_codes{CHUNKS - 1}", align_bytes=64)
+        y_scales = keep.tile([P, NQ], U8, name="y_scales", align_bytes=64)
+        y_bf = keep.tile([P, NQ * PACK], BF16, name="y_bf", tag=f"q_codes{LAST}", align_bytes=64)
+        y_woven = y_bf[:].rearrange("p (c t) -> p c t", t=PACK)
         for c in range(CHUNKS):
-            piece = y_bf[:, c * QC * PACK : (c + 1) * QC * PACK].rearrange("p (c t) -> p c t", t=PACK)
-            weave(nc.scalar.copy if c in SCALAR_WEAVES else nc.vector.tensor_copy, piece, y[c])
-        for first in range(0, NQ, NQ // 2):
-            cols = slice(first, first + NQ // 2)
-            quantize(y_codes[:, cols], y_scales[:, cols], y_bf[:, first * PACK : (first + NQ // 2) * PACK])
-            nc.sync.dma_start(out=y_words_hbm[:, cols], in_=y_codes[:, cols].bitcast(I32))
+            copy, w = (nc.scalar.copy, QC // 2) if c == LAST else (nc.vector.tensor_copy, QC)
+            for lo in range(0, QC, w):
+                first = c * QC + lo
+                weave(copy, y_woven[:, first : first + w, :], y[c][:, :, lo : lo + w])
+        for first in range(0, NQ, HALF):
+            cols = slice(first, first + HALF)
+            quantize(y_codes[:, cols], y_scales[:, cols], y_bf[:, first * PACK : (first + HALF) * PACK])
 
-        for quad in range(4):
-            queue = nc.scalar if quad % 2 else nc.sync
-            queue.dma_start(
-                out=y_scales_hbm[4 * quad : 4 * quad + 4, :],
-                in_=y_scales[32 * quad : 32 * quad + 4, :].bitcast(I32),
+        nc.sync.dma_start(
+            out=out_1[0].rearrange("p q t -> p (q t)").bitcast(I32), in_=y_codes[:].bitcast(I32)
+        )
+        scale_rows = out_2[0].bitcast(I32)
+        for quad in range(P // QUADRANT):
+            nc.scalar.dma_start(
+                out=scale_rows[PACK * quad : PACK * (quad + 1), :],
+                in_=y_scales[QUADRANT * quad : QUADRANT * quad + PACK, :].bitcast(I32),
             )

@@ -23,9 +23,8 @@ LIST_ROWS = 16
 QUADRANT = 32
 QC = 128
 CHUNKS = NQ // QC
-LAST = CHUNKS - 1
-Q_LOADS = (2 * QC, QC, QC)
 HALF = NQ // 2
+PAIR = 2
 
 
 def weave(copy, dst, src):
@@ -49,8 +48,8 @@ def tile_attend_plw_softf_f_topk_kernel(tc, qT, kT, ls, offs, out_0, out_1, out_
         ls_col = keep.tile([P, PACK], F32, name="ls_col")
         planes = [keep.tile([P, T], F32, name=f"plane{t}") for t in range(PACK)]
         q_raw = [
-            keep.tile([P, PACK, w], F32, name=f"q_raw{h}", tag=f"q_raw{h}", align_bytes=64)
-            for h, w in enumerate(Q_LOADS)
+            keep.tile([P, PACK, QC], F32, name=f"q_raw{c}", tag=f"q_raw{c}", align_bytes=64)
+            for c in range(CHUNKS)
         ]
         k_rows = kT.rearrange("(p t) n -> t p n", t=PACK)
         q_rows = qT[0].rearrange("(p t) n -> p t n", t=PACK)
@@ -59,11 +58,8 @@ def tile_attend_plw_softf_f_topk_kernel(tc, qT, kT, ls, offs, out_0, out_1, out_
         nc.scalar.dma_start(out=ls_col[:], in_=ls[0, 0].rearrange("(p c) -> p c", c=PACK))
         for t in range(1, PACK):
             nc.sync.dma_start(out=planes[t][:], in_=k_rows[t])
-        q_chunks = []
-        for h, w in enumerate(Q_LOADS):
-            first = sum(Q_LOADS[:h])
-            nc.sync.dma_start(out=q_raw[h][:], in_=q_rows[:, :, first : first + w])
-            q_chunks.extend(q_raw[h][:, :, lo : lo + QC] for lo in range(0, w, QC))
+        for c in range(CHUNKS):
+            nc.sync.dma_start(out=q_raw[c][:], in_=q_rows[:, :, c * QC : (c + 1) * QC])
 
         ident = keep.tile([P, P], F32, name="ident")
         make_identity(nc, ident[:])
@@ -92,83 +88,89 @@ def tile_attend_plw_softf_f_topk_kernel(tc, qT, kT, ls, offs, out_0, out_1, out_
         nc.vector.tensor_copy(out=k_dealt[:, :, :, 3], in_=planes[3][:].indirect(offsets[:]))
 
         q_bf = [keep.tile([P, QC, PACK], BF16, name=f"q_bf{c}", align_bytes=64) for c in range(CHUNKS)]
-        q_codes = [
-            keep.tile([P, QC], U32, name=f"q_codes{c}", tag=f"q_codes{c}", align_bytes=64)
-            for c in range(CHUNKS)
-        ]
         q_scales = [keep.tile([P, QC], U8, name=f"q_scales{c}", align_bytes=64) for c in range(CHUNKS)]
         k_scales = [keep.tile([P, P], U8, name=f"k_scales{r}", align_bytes=64) for r in range(PACK)]
+        q_codes, k_codes = {}, {}
 
-        def quantize_q(c):
+        def quantize_q(c, tag):
+            q_codes[c] = keep.tile([P, QC], U32, name=f"q_codes{c}", tag=tag, align_bytes=64)
             quantize(q_codes[c][:], q_scales[c][:], q_bf[c][:].rearrange("p c t -> p (c t)"))
 
-        for c in range(CHUNKS):
-            weave(nc.scalar.copy if c else nc.vector.tensor_copy, q_bf[c][:], q_chunks[c])
-        quantize_q(0)
-        k_words = keep.tile([P, N], U32, name="k_words", tag="q_raw0", align_bytes=64)
-        k_codes = [k_words[:, r * P : (r + 1) * P] for r in range(PACK)]
-        for r in range(PACK):
-            quantize(k_codes[r], k_scales[r][:], k_bf[:, r * P * PACK : (r + 1) * P * PACK])
-        for c in range(1, CHUNKS):
-            quantize_q(c)
+        def quantize_k(pair):
+            words = keep.tile([P, PAIR * P], U32, name=f"k_words{pair}", tag=f"q_raw{pair}", align_bytes=64)
+            for j in range(PAIR):
+                r = PAIR * pair + j
+                k_codes[r] = words[:, j * P : (j + 1) * P]
+                quantize(k_codes[r], k_scales[r][:], k_bf[:, r * P * PACK : (r + 1) * P * PACK])
 
-        scores = []
-        for c in range(CHUNKS):
-            tiles_a_bank = PACK if c else PACK // 2
-            banks = [
-                psum.tile([P, tiles_a_bank, QC], F32, name=f"scores{c}_{b}")
-                for b in range(PACK // tiles_a_bank)
-            ]
-            scores.append(banks)
-            for r in range(PACK):
-                nc.tensor.matmul_mx(
-                    out=banks[r // tiles_a_bank][:, r % tiles_a_bank, :],
-                    lhsT=k_codes[r].bitcast(FP8X4),
-                    lhsT_scale=k_scales[r][:],
-                    rhs=q_codes[c][:].bitcast(FP8X4),
-                    rhs_scale=q_scales[c][:],
-                    start=True,
-                    stop=True,
-                )
+        def matmul(out, r, c):
+            nc.tensor.matmul_mx(
+                out=out,
+                lhsT=k_codes[r].bitcast(FP8X4),
+                lhsT_scale=k_scales[r][:],
+                rhs=q_codes[c][:].bitcast(FP8X4),
+                rhs_scale=q_scales[c][:],
+                start=True,
+                stop=True,
+            )
 
         y_rows = out_0.rearrange("(p r) q -> p r q", r=PACK)
-        y_halves = [keep.tile([P, PACK, HALF], F32, name=f"y{h}") for h in range(NQ // HALF)]
-        y = [half[:, :, lo : lo + QC] for half in y_halves for lo in range(0, HALF, QC)]
+        y = [keep.tile([P, PACK, HALF], F32, name=f"y{h}") for h in range(NQ // HALF)]
+
+        def scores(tiles, chunks):
+            bank = psum.tile([P, len(tiles), len(chunks) * QC], F32, name=f"scores{tiles[0]}_{chunks[0]}")
+            for i, c in enumerate(chunks):
+                for j, r in enumerate(tiles):
+                    matmul(bank[:, j, i * QC : (i + 1) * QC], r, c)
+            return bank
+
+        def weights(bank, tiles, chunks):
+            first, w = chunks[0] * QC, len(chunks) * QC
+            shifted = keep.tile([P, len(tiles), w], F32, name=f"shifted{tiles[0]}_{chunks[0]}")
+            nc.vector.tensor_tensor(
+                out=shifted[:],
+                in0=bank[:],
+                in1=ls_all[:, first : first + w].unsqueeze(1).to_broadcast([P, len(tiles), w]),
+                op=SUB,
+            )
+            h, lo = divmod(first, HALF)
+            nc.scalar.activation(out=y[h][:, tiles[0] : tiles[-1] + 1, lo : lo + w], in_=shifted[:], func=EXP)
+
+        def store_y(h, pair):
+            rows = slice(PAIR * pair, PAIR * (pair + 1))
+            nc.sync.dma_start(out=y_rows[:, rows, h * HALF : (h + 1) * HALF], in_=y[h][:, rows, :])
+
         for c in range(CHUNKS):
-            tag = f"q_raw{len(Q_LOADS) - 1}" if c == 1 else f"shifted{c}"
-            shifted = keep.tile([P, PACK, QC], F32, name=f"shifted{c}", tag=tag, align_bytes=64)
-            tiles_a_bank = PACK // len(scores[c])
-            w = QC // 2 if c == LAST else QC
-            for lo in range(0, QC, w):
-                first = c * QC + lo
-                for b, bank in enumerate(scores[c]):
-                    nc.vector.tensor_tensor(
-                        out=shifted[:, b * tiles_a_bank : (b + 1) * tiles_a_bank, lo : lo + w],
-                        in0=bank[:, :, lo : lo + w],
-                        in1=ls_all[:, first : first + w].unsqueeze(1).to_broadcast([P, tiles_a_bank, w]),
-                        op=SUB,
-                    )
-                nc.scalar.activation(out=y[c][:, :, lo : lo + w], in_=shifted[:, :, lo : lo + w], func=EXP)
-            h, rest = divmod((c + 1) * QC, HALF)
-            if rest == 0:
-                nc.sync.dma_start(out=y_rows[:, :, (h - 1) * HALF : h * HALF], in_=y_halves[h - 1][:])
+            weave(nc.scalar.copy, q_bf[c][:], q_raw[c][:])
+        for pair in range(2):
+            quantize_q(pair, f"q_codes{pair}")
+            quantize_k(pair)
+        quantize_q(2, "q_codes2")
+        banks = [scores((0, 1), (0, 1)), scores((2, 3), (0, 1)), scores((0, 1, 2, 3), (2,))]
+        for pair in range(2):
+            weights(banks[pair], (PAIR * pair, PAIR * pair + 1), (0, 1))
+            store_y(0, pair)
+        quantize_q(3, "q_codes0")
+        last = [scores((0, 1), (3,)), scores((2, 3), (3,))]
+        weights(banks[2], (0, 1, 2, 3), (2,))
+        for pair in range(2):
+            weights(last[pair], (PAIR * pair, PAIR * pair + 1), (3,))
+            store_y(1, pair)
 
         y_codes = keep.tile([P, NQ], U32, name="y_codes", align_bytes=64)
         y_scales = keep.tile([P, NQ], U8, name="y_scales", align_bytes=64)
-        y_bf = keep.tile([P, NQ * PACK], BF16, name="y_bf", tag=f"q_codes{LAST}", align_bytes=64)
+        y_bf = keep.tile([P, NQ * PACK], BF16, name="y_bf", tag="q_codes0", align_bytes=64)
         y_woven = y_bf[:].rearrange("p (c t) -> p c t", t=PACK)
+        word_rows = out_1[0].rearrange("p q t -> p (q t)").bitcast(I32)
         for c in range(CHUNKS):
-            copy, w = (nc.scalar.copy, QC // 2) if c == LAST else (nc.vector.tensor_copy, QC)
-            for lo in range(0, QC, w):
-                first = c * QC + lo
-                weave(copy, y_woven[:, first : first + w, :], y[c][:, :, lo : lo + w])
+            h, lo = divmod(c * QC, HALF)
+            copy = nc.scalar.copy if c == CHUNKS - 1 else nc.vector.tensor_copy
+            weave(copy, y_woven[:, c * QC : (c + 1) * QC, :], y[h][:, :, lo : lo + QC])
         for first in range(0, NQ, HALF):
             cols = slice(first, first + HALF)
             quantize(y_codes[:, cols], y_scales[:, cols], y_bf[:, first * PACK : (first + HALF) * PACK])
+            nc.sync.dma_start(out=word_rows[:, cols], in_=y_codes[:, cols].bitcast(I32))
 
-        nc.sync.dma_start(
-            out=out_1[0].rearrange("p q t -> p (q t)").bitcast(I32), in_=y_codes[:].bitcast(I32)
-        )
         scale_rows = out_2[0].bitcast(I32)
         for quad in range(P // QUADRANT):
             nc.scalar.dma_start(

@@ -16,6 +16,8 @@ FP8X4 = mybir.dt.float8_e4m3fn_x4
 EXP = mybir.ActivationFunctionType.Exp
 COPY = mybir.ActivationFunctionType.Copy
 SUB = mybir.AluOpType.subtract
+MULT = mybir.AluOpType.mult
+ADD = mybir.AluOpType.add
 
 P = 128
 PACK = 4
@@ -23,8 +25,10 @@ LIST_ROWS = 16
 QUADRANT = 32
 QC = 128
 CHUNKS = NQ // QC
+LAST = CHUNKS - 1
 HALF = NQ // 2
 PAIR = 2
+RAW = PACK * QC * 4
 
 
 def weave(copy, dst, src):
@@ -42,15 +46,19 @@ def tile_attend_plw_softf_f_topk_kernel(tc, qT, kT, ls, offs, out_0, out_1, out_
 
     with ExitStack() as ctx:
         keep = ctx.enter_context(tc.tile_pool(name="keep", bufs=1))
+        reuse = ctx.enter_context(tc.tile_pool(name="reuse", bufs=1))
         psum = ctx.enter_context(tc.psum_pool(name="psum", bufs=1))
+
+        def placed(shape, dtype, name, offset):
+            return reuse.tile(shape, dtype, name=name, offset=offset, align_bytes=64)
+
+        raw_at = [(3 * c + 1) * RAW for c in range(CHUNKS)]
+        codes_at, bf_at = 12 * RAW, 16 * RAW
 
         offsets = keep.tile([P, N // LIST_ROWS], U16, name="offsets")
         ls_col = keep.tile([P, PACK], F32, name="ls_col")
         planes = [keep.tile([P, T], F32, name=f"plane{t}") for t in range(PACK)]
-        q_raw = [
-            keep.tile([P, PACK, QC], F32, name=f"q_raw{c}", tag=f"q_raw{c}", align_bytes=64)
-            for c in range(CHUNKS)
-        ]
+        q_raw = [placed([P, PACK, QC], F32, f"q_raw{c}", raw_at[c]) for c in range(CHUNKS)]
         k_rows = kT.rearrange("(p t) n -> t p n", t=PACK)
         q_rows = qT[0].rearrange("(p t) n -> p t n", t=PACK)
         nc.sync.dma_start(out=planes[0][:], in_=k_rows[0])
@@ -87,89 +95,88 @@ def tile_attend_plw_softf_f_topk_kernel(tc, qT, kT, ls, offs, out_0, out_1, out_
         nc.vector.tensor_copy(out=k_dealt[:, :, :, 2], in_=gathered2[:].rearrange("p (s r) -> p s r", r=PACK))
         nc.vector.tensor_copy(out=k_dealt[:, :, :, 3], in_=planes[3][:].indirect(offsets[:]))
 
-        q_bf = [keep.tile([P, QC, PACK], BF16, name=f"q_bf{c}", align_bytes=64) for c in range(CHUNKS)]
+        q_bf = [placed([P, QC, PACK], BF16, f"q_bf{c}", bf_at + c * RAW) for c in range(CHUNKS)]
         q_scales = [keep.tile([P, QC], U8, name=f"q_scales{c}", align_bytes=64) for c in range(CHUNKS)]
         k_scales = [keep.tile([P, P], U8, name=f"k_scales{r}", align_bytes=64) for r in range(PACK)]
-        q_codes, k_codes = {}, {}
+        q_codes = {}
 
-        def quantize_q(c, tag):
-            q_codes[c] = keep.tile([P, QC], U32, name=f"q_codes{c}", tag=tag, align_bytes=64)
+        def quantize_q(c, offset):
+            q_codes[c] = placed([P, QC], U32, f"q_codes{c}", offset)
             quantize(q_codes[c][:], q_scales[c][:], q_bf[c][:].rearrange("p c t -> p (c t)"))
-
-        def quantize_k(pair):
-            words = keep.tile([P, PAIR * P], U32, name=f"k_words{pair}", tag=f"q_raw{pair}", align_bytes=64)
-            for j in range(PAIR):
-                r = PAIR * pair + j
-                k_codes[r] = words[:, j * P : (j + 1) * P]
-                quantize(k_codes[r], k_scales[r][:], k_bf[:, r * P * PACK : (r + 1) * P * PACK])
-
-        def matmul(out, r, c):
-            nc.tensor.matmul_mx(
-                out=out,
-                lhsT=k_codes[r].bitcast(FP8X4),
-                lhsT_scale=k_scales[r][:],
-                rhs=q_codes[c][:].bitcast(FP8X4),
-                rhs_scale=q_scales[c][:],
-                start=True,
-                stop=True,
-            )
 
         y_rows = out_0.rearrange("(p r) q -> p r q", r=PACK)
         y = [keep.tile([P, PACK, HALF], F32, name=f"y{h}") for h in range(NQ // HALF)]
 
-        def scores(tiles, chunks):
-            bank = psum.tile([P, len(tiles), len(chunks) * QC], F32, name=f"scores{tiles[0]}_{chunks[0]}")
-            for i, c in enumerate(chunks):
-                for j, r in enumerate(tiles):
-                    matmul(bank[:, j, i * QC : (i + 1) * QC], r, c)
+        def scores(c, tiles):
+            bank = psum.tile([P, len(tiles), QC], F32, name=f"scores{c}_{tiles[0]}")
+            for j, r in enumerate(tiles):
+                nc.tensor.matmul_mx(
+                    out=bank[:, j, :],
+                    lhsT=k_words[:, r * P : (r + 1) * P].bitcast(FP8X4),
+                    lhsT_scale=k_scales[r][:],
+                    rhs=q_codes[c][:].bitcast(FP8X4),
+                    rhs_scale=q_scales[c][:],
+                    start=True,
+                    stop=True,
+                )
             return bank
 
-        def weights(bank, tiles, chunks):
-            first, w = chunks[0] * QC, len(chunks) * QC
-            shifted = keep.tile([P, len(tiles), w], F32, name=f"shifted{tiles[0]}_{chunks[0]}")
+        def weights(bank, c, tiles, shifted):
             nc.vector.tensor_tensor(
                 out=shifted[:],
                 in0=bank[:],
-                in1=ls_all[:, first : first + w].unsqueeze(1).to_broadcast([P, len(tiles), w]),
+                in1=ls_all[:, c * QC : (c + 1) * QC].unsqueeze(1).to_broadcast([P, len(tiles), QC]),
                 op=SUB,
             )
-            h, lo = divmod(first, HALF)
-            nc.scalar.activation(out=y[h][:, tiles[0] : tiles[-1] + 1, lo : lo + w], in_=shifted[:], func=EXP)
+            h, lo = divmod(c * QC, HALF)
+            nc.scalar.activation(out=y[h][:, tiles[0] : tiles[-1] + 1, lo : lo + QC], in_=shifted[:], func=EXP)
 
-        def store_y(h, pair):
-            rows = slice(PAIR * pair, PAIR * (pair + 1))
-            nc.sync.dma_start(out=y_rows[:, rows, h * HALF : (h + 1) * HALF], in_=y[h][:, rows, :])
+        def store_y(h, rows, cols):
+            nc.sync.dma_start(
+                out=y_rows[:, rows, h * HALF + cols.start : h * HALF + cols.stop], in_=y[h][:, rows, cols]
+            )
 
+        low, high, every = (0, 1), (2, 3), (0, 1, 2, 3)
         for c in range(CHUNKS):
             weave(nc.scalar.copy, q_bf[c][:], q_raw[c][:])
-        for pair in range(2):
-            quantize_q(pair, f"q_codes{pair}")
-            quantize_k(pair)
-        quantize_q(2, "q_codes2")
-        banks = [scores((0, 1), (0, 1)), scores((2, 3), (0, 1)), scores((0, 1, 2, 3), (2,))]
-        for pair in range(2):
-            weights(banks[pair], (PAIR * pair, PAIR * pair + 1), (0, 1))
-            store_y(0, pair)
-        quantize_q(3, "q_codes0")
-        last = [scores((0, 1), (3,)), scores((2, 3), (3,))]
-        weights(banks[2], (0, 1, 2, 3), (2,))
-        for pair in range(2):
-            weights(last[pair], (PAIR * pair, PAIR * pair + 1), (3,))
-            store_y(1, pair)
+        quantize_q(0, codes_at)
+        k_words = placed([P, N], U32, "k_words", raw_at[0])
+        for r in range(PACK):
+            quantize(k_words[:, r * P : (r + 1) * P], k_scales[r][:], k_bf[:, r * P * PACK : (r + 1) * P * PACK])
+        quantize_q(1, codes_at + RAW)
+        banks = [scores(0, low), scores(0, high), scores(1, every)]
+        weights(banks[0], 0, low, keep.tile([P, PAIR, QC], F32, name="shifted0"))
+        quantize_q(2, codes_at + 2 * RAW)
+        bank2 = scores(2, every)
+        weights(banks[1], 0, high, placed([P, PAIR, QC], F32, "shifted1", raw_at[2] - RAW // 4))
+        store_y(0, slice(0, PACK), slice(0, QC))
+        weights(banks[2], 1, every, placed([P, PACK, QC], F32, "shifted2", raw_at[2] + RAW // 2))
+        store_y(0, slice(0, PACK), slice(QC, HALF))
+        quantize_q(LAST, codes_at + RAW)
+        last = [scores(LAST, low), scores(LAST, high)]
+        weights(bank2, 2, every, placed([P, PACK, QC], F32, "shifted3", raw_at[LAST]))
+        for pair, tiles in enumerate((low, high)):
+            weights(last[pair], LAST, tiles, keep.tile([P, PAIR, QC], F32, name=f"shifted4_{pair}"))
+            store_y(1, slice(PAIR * pair, PAIR * (pair + 1)), slice(0, HALF))
 
         y_codes = keep.tile([P, NQ], U32, name="y_codes", align_bytes=64)
         y_scales = keep.tile([P, NQ], U8, name="y_scales", align_bytes=64)
-        y_bf = keep.tile([P, NQ * PACK], BF16, name="y_bf", tag="q_codes0", align_bytes=64)
-        y_woven = y_bf[:].rearrange("p (c t) -> p c t", t=PACK)
+        y_bf0 = placed([P, QC, PACK], BF16, "y_bf0", codes_at + RAW - RAW // 2 + 64)
+        y_bf = placed([P, LAST * QC, PACK], BF16, "y_bf", codes_at + RAW + 64)
         word_rows = out_1[0].rearrange("p q t -> p (q t)").bitcast(I32)
-        for c in range(CHUNKS):
+        weave(nc.vector.tensor_copy, y_bf0[:], y[0][:, :, 0:QC])
+        for c in range(1, CHUNKS):
             h, lo = divmod(c * QC, HALF)
-            copy = nc.scalar.copy if c == CHUNKS - 1 else nc.vector.tensor_copy
-            weave(copy, y_woven[:, c * QC : (c + 1) * QC, :], y[h][:, :, lo : lo + QC])
-        for first in range(0, NQ, HALF):
-            cols = slice(first, first + HALF)
-            quantize(y_codes[:, cols], y_scales[:, cols], y_bf[:, first * PACK : (first + HALF) * PACK])
-            nc.sync.dma_start(out=word_rows[:, cols], in_=y_codes[:, cols].bitcast(I32))
+            copy = nc.scalar.copy if c == LAST else nc.vector.tensor_copy
+            weave(copy, y_bf[:, (c - 1) * QC : c * QC, :], y[h][:, :, lo : lo + QC])
+            values = y_bf0[:] if c == 1 else y_bf[:, (c - 2) * QC : (c - 1) * QC, :]
+            cols = slice((c - 1) * QC, c * QC)
+            quantize(y_codes[:, cols], y_scales[:, cols], values.rearrange("p c t -> p (c t)"))
+            if c == 2:
+                nc.sync.dma_start(out=word_rows[:, 0:HALF], in_=y_codes[:, 0:HALF].bitcast(I32))
+        cols = slice(LAST * QC, NQ)
+        quantize(y_codes[:, cols], y_scales[:, cols], y_bf[:, (LAST - 1) * QC :, :].rearrange("p c t -> p (c t)"))
+        nc.sync.dma_start(out=word_rows[:, HALF:], in_=y_codes[:, HALF:].bitcast(I32))
 
         scale_rows = out_2[0].bitcast(I32)
         for quad in range(P // QUADRANT):

@@ -107,29 +107,31 @@ def tile_attend_plw_softf_f_topk_kernel(tc, qT, kT, ls, offs, out_0, out_1, out_
         y_rows = out_0.rearrange("(p r) q -> p r q", r=PACK)
         y = [keep.tile([P, PACK, HALF], F32, name=f"y{h}") for h in range(NQ // HALF)]
 
-        def scores(c, tiles):
-            bank = psum.tile([P, len(tiles), QC], F32, name=f"scores{c}_{tiles[0]}")
-            for j, r in enumerate(tiles):
-                nc.tensor.matmul_mx(
-                    out=bank[:, j, :],
-                    lhsT=k_words[:, r * P : (r + 1) * P].bitcast(FP8X4),
-                    lhsT_scale=k_scales[r][:],
-                    rhs=q_codes[c][:].bitcast(FP8X4),
-                    rhs_scale=q_scales[c][:],
-                    start=True,
-                    stop=True,
-                )
+        def scores(chunks, tiles):
+            bank = psum.tile([P, len(tiles), len(chunks) * QC], F32, name=f"scores{chunks[0]}_{tiles[0]}")
+            for i, c in enumerate(chunks):
+                for j, r in enumerate(tiles):
+                    nc.tensor.matmul_mx(
+                        out=bank[:, j, i * QC : (i + 1) * QC],
+                        lhsT=k_words[:, r * P : (r + 1) * P].bitcast(FP8X4),
+                        lhsT_scale=k_scales[r][:],
+                        rhs=q_codes[c][:].bitcast(FP8X4),
+                        rhs_scale=q_scales[c][:],
+                        start=True,
+                        stop=True,
+                    )
             return bank
 
-        def weights(bank, c, tiles, shifted):
+        def weights(bank, chunks, tiles, shifted):
+            first, w = chunks[0] * QC, len(chunks) * QC
             nc.vector.tensor_tensor(
                 out=shifted[:],
                 in0=bank[:],
-                in1=ls_all[:, c * QC : (c + 1) * QC].unsqueeze(1).to_broadcast([P, len(tiles), QC]),
+                in1=ls_all[:, first : first + w].unsqueeze(1).to_broadcast([P, len(tiles), w]),
                 op=SUB,
             )
-            h, lo = divmod(c * QC, HALF)
-            nc.scalar.activation(out=y[h][:, tiles[0] : tiles[-1] + 1, lo : lo + QC], in_=shifted[:], func=EXP)
+            h, lo = divmod(first, HALF)
+            nc.scalar.activation(out=y[h][:, tiles[0] : tiles[-1] + 1, lo : lo + w], in_=shifted[:], func=EXP)
 
         def store_y(h, rows, cols):
             nc.sync.dma_start(
@@ -144,43 +146,50 @@ def tile_attend_plw_softf_f_topk_kernel(tc, qT, kT, ls, offs, out_0, out_1, out_
         for r in range(PACK):
             quantize(k_words[:, r * P : (r + 1) * P], k_scales[r][:], k_bf[:, r * P * PACK : (r + 1) * P * PACK])
         quantize_q(1, codes_at + RAW)
-        banks = [scores(0, low), scores(0, high), scores(1, every)]
-        weights(banks[0], 0, low, keep.tile([P, PAIR, QC], F32, name="shifted0"))
+        banks = [scores((0,), low), scores((1,), low), scores((0, 1), high)]
+        weights(banks[0], (0,), low, keep.tile([P, PAIR, QC], F32, name="shifted0"))
         quantize_q(2, codes_at + 2 * RAW)
-        bank2 = scores(2, every)
-        weights(banks[1], 0, high, placed([P, PAIR, QC], F32, "shifted1", raw_at[2] - RAW // 4))
-        store_y(0, slice(0, PACK), slice(0, QC))
-        weights(banks[2], 1, every, placed([P, PACK, QC], F32, "shifted2", raw_at[2] + RAW // 2))
-        store_y(0, slice(0, PACK), slice(QC, HALF))
+        bank2 = scores((2,), every)
+        weights(banks[1], (1,), low, placed([P, PAIR, QC], F32, "shifted1", raw_at[2] - RAW // 4))
+        store_y(0, slice(0, PAIR), slice(0, HALF))
+        weights(banks[2], (0, 1), high, placed([P, PAIR, HALF], F32, "shifted2", raw_at[2] + RAW // 2))
+        store_y(0, slice(PAIR, PACK), slice(0, HALF))
         quantize_q(LAST, codes_at + RAW)
-        last = [scores(LAST, low), scores(LAST, high)]
-        weights(bank2, 2, every, placed([P, PACK, QC], F32, "shifted3", raw_at[LAST]))
+        last = [scores((LAST,), low), scores((LAST,), high)]
+        weights(bank2, (2,), every, placed([P, PACK, QC], F32, "shifted3", raw_at[LAST]))
         for pair, tiles in enumerate((low, high)):
-            weights(last[pair], LAST, tiles, keep.tile([P, PAIR, QC], F32, name=f"shifted4_{pair}"))
+            weights(last[pair], (LAST,), tiles, keep.tile([P, PAIR, QC], F32, name=f"shifted4_{pair}"))
             store_y(1, slice(PAIR * pair, PAIR * (pair + 1)), slice(0, HALF))
 
         y_codes = keep.tile([P, NQ], U32, name="y_codes", align_bytes=64)
         y_scales = keep.tile([P, NQ], U8, name="y_scales", align_bytes=64)
-        y_bf0 = placed([P, QC, PACK], BF16, "y_bf0", codes_at + RAW - RAW // 2 + 64)
+        y_bf0 = placed([P, QC, PACK], BF16, "y_bf0", bf_at + LAST * RAW)
         y_bf = placed([P, LAST * QC, PACK], BF16, "y_bf", codes_at + RAW + 64)
         word_rows = out_1[0].rearrange("p q t -> p (q t)").bitcast(I32)
-        weave(nc.vector.tensor_copy, y_bf0[:], y[0][:, :, 0:QC])
-        for c in range(1, CHUNKS):
-            h, lo = divmod(c * QC, HALF)
-            copy = nc.scalar.copy if c == LAST else nc.vector.tensor_copy
-            weave(copy, y_bf[:, (c - 1) * QC : c * QC, :], y[h][:, :, lo : lo + QC])
-            values = y_bf0[:] if c == 1 else y_bf[:, (c - 2) * QC : (c - 1) * QC, :]
-            cols = slice((c - 1) * QC, c * QC)
+        nc.gpsimd.tensor_scalar(
+            out=y_bf0[:], in0=y[0][:, :, 0:QC].rearrange("p t c -> p c t"), scalar1=1.0, scalar2=0.0, op0=MULT, op1=ADD
+        )
+
+        def quantize_y(c):
+            values = y_bf[:, (c - 1) * QC : c * QC, :] if c else y_bf0[:]
+            cols = slice(c * QC, (c + 1) * QC)
             quantize(y_codes[:, cols], y_scales[:, cols], values.rearrange("p c t -> p (c t)"))
-            if c == 2:
-                nc.sync.dma_start(out=word_rows[:, 0:HALF], in_=y_codes[:, 0:HALF].bitcast(I32))
-        cols = slice(LAST * QC, NQ)
-        quantize(y_codes[:, cols], y_scales[:, cols], y_bf[:, (LAST - 1) * QC :, :].rearrange("p c t -> p (c t)"))
+
+        weave(nc.vector.tensor_copy, y_bf[:, 0:QC, :], y[0][:, :, QC:])
+        weave(nc.vector.tensor_copy, y_bf[:, QC : 2 * QC, :], y[1][:, :, 0:QC])
+        quantize_y(0)
+        quantize_y(1)
+        nc.sync.dma_start(out=word_rows[:, 0:HALF], in_=y_codes[:, 0:HALF].bitcast(I32))
+        split = 80
+        weave(nc.vector.tensor_copy, y_bf[:, 2 * QC : 2 * QC + split, :], y[1][:, :, QC : QC + split])
+        weave(nc.scalar.copy, y_bf[:, 2 * QC + split :, :], y[1][:, :, QC + split :])
+        quantize_y(2)
+        quantize_y(LAST)
         nc.sync.dma_start(out=word_rows[:, HALF:], in_=y_codes[:, HALF:].bitcast(I32))
 
         scale_rows = out_2[0].bitcast(I32)
         for quad in range(P // QUADRANT):
-            nc.scalar.dma_start(
+            (nc.sync if quad % 2 else nc.scalar).dma_start(
                 out=scale_rows[PACK * quad : PACK * (quad + 1), :],
                 in_=y_scales[QUADRANT * quad : QUADRANT * quad + PACK, :].bitcast(I32),
             )

@@ -163,12 +163,10 @@ def tile_attend_plw_softf_f_topk_kernel(tc, qT, kT, ls, offs, out_0, out_1, out_
 
         y_codes = keep.tile([P, NQ], U32, name="y_codes", align_bytes=64)
         y_scales = keep.tile([P, NQ], U8, name="y_scales", align_bytes=64)
-        y_bf0 = placed([P, QC, PACK], BF16, "y_bf0", bf_at + LAST * RAW)
+        y_bf0 = placed([P, QC, PACK], BF16, "y_bf0", codes_at + RAW - RAW // 2 + 64)
         y_bf = placed([P, LAST * QC, PACK], BF16, "y_bf", codes_at + RAW + 64)
         word_rows = out_1[0].rearrange("p q t -> p (q t)").bitcast(I32)
-        nc.gpsimd.tensor_scalar(
-            out=y_bf0[:], in0=y[0][:, :, 0:QC].rearrange("p t c -> p c t"), scalar1=1.0, scalar2=0.0, op0=MULT, op1=ADD
-        )
+        weave(nc.vector.tensor_copy, y_bf0[:], y[0][:, :, 0:QC])
 
         def quantize_y(c):
             values = y_bf[:, (c - 1) * QC : c * QC, :] if c else y_bf0[:]

@@ -146,14 +146,14 @@ def tile_attend_plw_softf_f_topk_kernel(tc, qT, kT, ls, offs, out_0, out_1, out_
         for r in range(PACK):
             quantize(k_words[:, r * P : (r + 1) * P], k_scales[r][:], k_bf[:, r * P * PACK : (r + 1) * P * PACK])
         quantize_q(1, codes_at + RAW)
-        banks = [scores((0,), low), scores((1,), low), scores((0, 1), high)]
+        banks = [scores((0,), low), scores((0,), high), scores((1,), every)]
         weights(banks[0], (0,), low, keep.tile([P, PAIR, QC], F32, name="shifted0"))
         quantize_q(2, codes_at + 2 * RAW)
         bank2 = scores((2,), every)
-        weights(banks[1], (1,), low, placed([P, PAIR, QC], F32, "shifted1", raw_at[2] - RAW // 4))
-        store_y(0, slice(0, PAIR), slice(0, HALF))
-        weights(banks[2], (0, 1), high, placed([P, PAIR, HALF], F32, "shifted2", raw_at[2] + RAW // 2))
-        store_y(0, slice(PAIR, PACK), slice(0, HALF))
+        weights(banks[1], (0,), high, placed([P, PAIR, QC], F32, "shifted1", raw_at[2] - RAW // 4))
+        store_y(0, slice(0, PACK), slice(0, QC))
+        weights(banks[2], (1,), every, placed([P, PACK, QC], F32, "shifted2", raw_at[2] + RAW // 2))
+        store_y(0, slice(0, PACK), slice(QC, HALF))
         quantize_q(LAST, codes_at + RAW)
         last = [scores((LAST,), low), scores((LAST,), high)]
         weights(bank2, (2,), every, placed([P, PACK, QC], F32, "shifted3", raw_at[LAST]))

@@ -187,7 +187,7 @@ def tile_attend_plw_softf_f_topk_kernel(tc, qT, kT, ls, offs, out_0, out_1, out_
 
         scale_rows = out_2[0].bitcast(I32)
         for quad in range(P // QUADRANT):
-            (nc.sync if quad % 2 else nc.scalar).dma_start(
+            nc.scalar.dma_start(
                 out=scale_rows[PACK * quad : PACK * (quad + 1), :],
                 in_=y_scales[QUADRANT * quad : QUADRANT * quad + PACK, :].bitcast(I32),
             )

@@ -90,9 +90,7 @@ def tile_attend_plw_softf_f_topk_kernel(tc, qT, kT, ls, offs, out_0, out_1, out_
             out=k_dealt[:, :, :, 0:2].rearrange("p s r t -> p s t r"),
             in_=gathered01[:].rearrange("p t (s r) -> p s t r", r=PACK),
         )
-        gathered2 = keep.tile([P, N], BF16, name="gathered2")
-        nc.vector.tensor_copy(out=gathered2[:], in_=planes[2][:].indirect(offsets[:]))
-        nc.vector.tensor_copy(out=k_dealt[:, :, :, 2], in_=gathered2[:].rearrange("p (s r) -> p s r", r=PACK))
+        nc.vector.tensor_copy(out=k_dealt[:, :, :, 2], in_=planes[2][:].indirect(offsets[:]))
         nc.vector.tensor_copy(out=k_dealt[:, :, :, 3], in_=planes[3][:].indirect(offsets[:]))
 
         q_bf = [placed([P, QC, PACK], BF16, f"q_bf{c}", bf_at + c * RAW) for c in range(CHUNKS)]
@@ -177,7 +175,7 @@ def tile_attend_plw_softf_f_topk_kernel(tc, qT, kT, ls, offs, out_0, out_1, out_
         weave(nc.vector.tensor_copy, y_bf[:, QC : 2 * QC, :], y[1][:, :, 0:QC])
         quantize_y(0)
         quantize_y(1)
-        nc.sync.dma_start(out=word_rows[:, 0:HALF], in_=y_codes[:, 0:HALF].bitcast(I32))
+        nc.scalar.dma_start(out=word_rows[:, 0:HALF], in_=y_codes[:, 0:HALF].bitcast(I32))
         split = 80
         weave(nc.vector.tensor_copy, y_bf[:, 2 * QC : 2 * QC + split, :], y[1][:, :, QC : QC + split])
         weave(nc.scalar.copy, y_bf[:, 2 * QC + split :, :], y[1][:, :, QC + split :])

@@ -147,14 +147,15 @@ def tile_attend_plw_softf_f_topk_kernel(tc, qT, kT, ls, offs, out_0, out_1, out_
         banks = [scores((0,), low), scores((0,), high), scores((1,), every)]
         weights(banks[0], (0,), low, keep.tile([P, PAIR, QC], F32, name="shifted0"))
         quantize_q(2, codes_at + 2 * RAW)
-        bank2 = scores((2,), every)
+        bank2 = [scores((2,), low), scores((2,), high)]
         weights(banks[1], (0,), high, placed([P, PAIR, QC], F32, "shifted1", raw_at[2] - RAW // 4))
         store_y(0, slice(0, PACK), slice(0, QC))
         weights(banks[2], (1,), every, placed([P, PACK, QC], F32, "shifted2", raw_at[2] + RAW // 2))
         store_y(0, slice(0, PACK), slice(QC, HALF))
         quantize_q(LAST, codes_at + RAW)
         last = [scores((LAST,), low), scores((LAST,), high)]
-        weights(bank2, (2,), every, placed([P, PACK, QC], F32, "shifted3", raw_at[LAST]))
+        for pair, tiles in enumerate((low, high)):
+            weights(bank2[pair], (2,), tiles, placed([P, PAIR, QC], F32, f"shifted3_{pair}", raw_at[LAST] + pair * RAW // 2))
         for pair, tiles in enumerate((low, high)):
             weights(last[pair], (LAST,), tiles, keep.tile([P, PAIR, QC], F32, name=f"shifted4_{pair}"))
             store_y(1, slice(PAIR * pair, PAIR * (pair + 1)), slice(0, HALF))
@@ -176,7 +177,7 @@ def tile_attend_plw_softf_f_topk_kernel(tc, qT, kT, ls, offs, out_0, out_1, out_
         quantize_y(0)
         quantize_y(1)
         nc.scalar.dma_start(out=word_rows[:, 0:HALF], in_=y_codes[:, 0:HALF].bitcast(I32))
-        split = 80
+        split = 64
         weave(nc.vector.tensor_copy, y_bf[:, 2 * QC : 2 * QC + split, :], y[1][:, :, QC : QC + split])
         weave(nc.scalar.copy, y_bf[:, 2 * QC + split :, :], y[1][:, :, QC + split :])
         quantize_y(2)

@@ -83,15 +83,8 @@ def tile_attend_plw_softf_f_topk_kernel(tc, qT, kT, ls, offs, out_0, out_1, out_
 
         k_bf = keep.tile([P, N * PACK], BF16, name="k_bf", align_bytes=64)
         k_dealt = k_bf[:].rearrange("p (r s t) -> p s r t", r=PACK, t=PACK)
-        gathered01 = keep.tile([P, 2, N], BF16, name="gathered01")
-        for t in range(2):
-            nc.vector.tensor_copy(out=gathered01[:, t, :], in_=planes[t][:].indirect(offsets[:]))
-        nc.scalar.copy(
-            out=k_dealt[:, :, :, 0:2].rearrange("p s r t -> p s t r"),
-            in_=gathered01[:].rearrange("p t (s r) -> p s t r", r=PACK),
-        )
-        nc.vector.tensor_copy(out=k_dealt[:, :, :, 2], in_=planes[2][:].indirect(offsets[:]))
-        nc.vector.tensor_copy(out=k_dealt[:, :, :, 3], in_=planes[3][:].indirect(offsets[:]))
+        for t in range(PACK):
+            nc.vector.tensor_copy(out=k_dealt[:, :, :, t], in_=planes[t][:].indirect(offsets[:]))
 
         q_bf = [placed([P, QC, PACK], BF16, f"q_bf{c}", bf_at + c * RAW) for c in range(CHUNKS)]
         q_scales = [keep.tile([P, QC], U8, name=f"q_scales{c}", align_bytes=64) for c in range(CHUNKS)]
@@ -162,10 +155,12 @@ def tile_attend_plw_softf_f_topk_kernel(tc, qT, kT, ls, offs, out_0, out_1, out_
 
         y_codes = keep.tile([P, NQ], U32, name="y_codes", align_bytes=64)
         y_scales = keep.tile([P, NQ], U8, name="y_scales", align_bytes=64)
-        y_bf0 = placed([P, QC, PACK], BF16, "y_bf0", codes_at + RAW - RAW // 2 + 64)
+        y_bf0 = placed([P, QC, PACK], BF16, "y_bf0", bf_at + LAST * RAW)
         y_bf = placed([P, LAST * QC, PACK], BF16, "y_bf", codes_at + RAW + 64)
         word_rows = out_1[0].rearrange("p q t -> p (q t)").bitcast(I32)
-        weave(nc.vector.tensor_copy, y_bf0[:], y[0][:, :, 0:QC])
+        nc.gpsimd.tensor_scalar(
+            out=y_bf0[:], in0=y[0][:, :, 0:QC].rearrange("p t c -> p c t"), scalar1=1.0, scalar2=0.0, op0=MULT, op1=ADD
+        )
 
         def quantize_y(c):
             values = y_bf[:, (c - 1) * QC : c * QC, :] if c else y_bf0[:]

@@ -28,7 +28,8 @@ CHUNKS = NQ // QC
 LAST = CHUNKS - 1
 HALF = NQ // 2
 PAIR = 2
-RAW = PACK * QC * 4
+ROOM = 8192
+LOW, HIGH = slice(0, PAIR), slice(PAIR, PACK)
 
 
 def weave(copy, dst, src):
@@ -42,23 +43,23 @@ def tile_attend_plw_softf_f_topk_kernel(tc, qT, kT, ls, offs, out_0, out_1, out_
     nc = tc.nc
 
     def quantize(codes, scales, values):
-        nc.vector.quantize_mx(out=codes.bitcast(FP8X4), scales=scales, in_=values)
+        nc.vector.quantize_mx(out=codes.bitcast(FP8X4), scales=scales, in_=values.rearrange("p c t -> p (c t)"))
+
+    def gpsimd_copy(out, in_):
+        nc.gpsimd.tensor_scalar(out=out, in0=in_, scalar1=1.0, scalar2=0.0, op0=MULT, op1=ADD)
 
     with ExitStack() as ctx:
         keep = ctx.enter_context(tc.tile_pool(name="keep", bufs=1))
         reuse = ctx.enter_context(tc.tile_pool(name="reuse", bufs=1))
         psum = ctx.enter_context(tc.psum_pool(name="psum", bufs=1))
 
-        def placed(shape, dtype, name, offset):
-            return reuse.tile(shape, dtype, name=name, offset=offset, align_bytes=64)
-
-        raw_at = [(3 * c + 1) * RAW for c in range(CHUNKS)]
-        codes_at, bf_at = 12 * RAW, 16 * RAW
+        def placed(shape, dtype, name, room, byte=0):
+            return reuse.tile(shape, dtype, name=name, offset=room * ROOM + byte, align_bytes=64)
 
         offsets = keep.tile([P, N // LIST_ROWS], U16, name="offsets")
         ls_col = keep.tile([P, PACK], F32, name="ls_col")
         planes = [keep.tile([P, T], F32, name=f"plane{t}") for t in range(PACK)]
-        q_raw = [placed([P, PACK, QC], F32, f"q_raw{c}", raw_at[c]) for c in range(CHUNKS)]
+        q_raw = [placed([P, PACK, QC], F32, f"q_raw{c}", (0, 1, 16, 2)[c]) for c in range(CHUNKS)]
         k_rows = kT.rearrange("(p t) n -> t p n", t=PACK)
         q_rows = qT[0].rearrange("(p t) n -> p t n", t=PACK)
         nc.sync.dma_start(out=planes[0][:], in_=k_rows[0])
@@ -71,7 +72,7 @@ def tile_attend_plw_softf_f_topk_kernel(tc, qT, kT, ls, offs, out_0, out_1, out_
 
         ident = keep.tile([P, P], F32, name="ident")
         make_identity(nc, ident[:])
-        ls_ps = psum.tile([P, PACK, P], F32, name="ls_ps")
+        ls_ps = psum.tile([P, PACK, P], F32, name="ls_ps", tag="bank7")
         for c in range(PACK):
             nc.tensor.transpose(ls_ps[:, c, :], ls_col[:, c : c + 1].to_broadcast([P, P]), ident[:])
         ls_all = keep.tile([P, NQ], F32, name="ls_all")
@@ -81,29 +82,32 @@ def tile_attend_plw_softf_f_topk_kernel(tc, qT, kT, ls, offs, out_0, out_1, out_
             func=COPY,
         )
 
-        k_bf = keep.tile([P, N * PACK], BF16, name="k_bf", align_bytes=64)
-        k_dealt = k_bf[:].rearrange("p (r s t) -> p s r t", r=PACK, t=PACK)
+        k_bf = keep.tile([P, PACK, P, PACK], BF16, name="k_bf", align_bytes=64)
+        k_dealt = k_bf[:].rearrange("p r s t -> p s r t")
         for t in range(PACK):
             nc.vector.tensor_copy(out=k_dealt[:, :, :, t], in_=planes[t][:].indirect(offsets[:]))
 
-        q_bf = [placed([P, QC, PACK], BF16, f"q_bf{c}", bf_at + c * RAW) for c in range(CHUNKS)]
         q_scales = [keep.tile([P, QC], U8, name=f"q_scales{c}", align_bytes=64) for c in range(CHUNKS)]
         k_scales = [keep.tile([P, P], U8, name=f"k_scales{r}", align_bytes=64) for r in range(PACK)]
-        q_codes = {}
-
-        def quantize_q(c, offset):
-            q_codes[c] = placed([P, QC], U32, f"q_codes{c}", offset)
-            quantize(q_codes[c][:], q_scales[c][:], q_bf[c][:].rearrange("p c t -> p (c t)"))
-
         y_rows = out_0.rearrange("(p r) q -> p r q", r=PACK)
         y = [keep.tile([P, PACK, HALF], F32, name=f"y{h}") for h in range(NQ // HALF)]
+        q_bf, q_codes, banks = {}, {}, {}
 
-        def scores(chunks, tiles):
-            bank = psum.tile([P, len(tiles), len(chunks) * QC], F32, name=f"scores{chunks[0]}_{tiles[0]}")
-            for i, c in enumerate(chunks):
-                for j, r in enumerate(tiles):
+        def weave_q(copy, c, src, room, byte=0):
+            q_bf[c] = placed([P, QC, PACK], BF16, f"q_bf{c}", room, byte)
+            weave(copy, q_bf[c][:], src)
+
+        def quantize_q(c, room, byte=0):
+            q_codes[c] = placed([P, QC], U32, f"q_codes{c}", room, byte)
+            quantize(q_codes[c][:], q_scales[c][:], q_bf[c][:])
+
+        def scores(c):
+            for pair, tiles in enumerate((LOW, HIGH)):
+                u = PAIR * c + pair
+                banks[u] = psum.tile([P, PAIR, QC], F32, name=f"scores{u}", tag=f"bank{u}")
+                for r in range(tiles.start, tiles.stop):
                     nc.tensor.matmul_mx(
-                        out=bank[:, j, i * QC : (i + 1) * QC],
+                        out=banks[u][:, r - tiles.start, :],
                         lhsT=k_words[:, r * P : (r + 1) * P].bitcast(FP8X4),
                         lhsT_scale=k_scales[r][:],
                         rhs=q_codes[c][:].bitcast(FP8X4),
@@ -111,70 +115,77 @@ def tile_attend_plw_softf_f_topk_kernel(tc, qT, kT, ls, offs, out_0, out_1, out_
                         start=True,
                         stop=True,
                     )
-            return bank
 
-        def weights(bank, chunks, tiles, shifted):
-            first, w = chunks[0] * QC, len(chunks) * QC
+        def y_part(c, tiles):
+            h, lo = divmod(c * QC, HALF)
+            return y[h][:, tiles, lo : lo + QC]
+
+        def weights(c, pair, room, byte=0):
+            u = PAIR * c + pair
+            shifted = placed([P, PAIR, QC], F32, f"shifted{u}", room, byte)
             nc.vector.tensor_tensor(
                 out=shifted[:],
-                in0=bank[:],
-                in1=ls_all[:, first : first + w].unsqueeze(1).to_broadcast([P, len(tiles), w]),
+                in0=banks[u][:],
+                in1=ls_all[:, c * QC : (c + 1) * QC].unsqueeze(1).to_broadcast([P, PAIR, QC]),
                 op=SUB,
             )
-            h, lo = divmod(first, HALF)
-            nc.scalar.activation(out=y[h][:, tiles[0] : tiles[-1] + 1, lo : lo + w], in_=shifted[:], func=EXP)
+            nc.scalar.activation(out=y_part(c, (LOW, HIGH)[pair]), in_=shifted[:], func=EXP)
 
-        def store_y(h, rows, cols):
-            nc.sync.dma_start(
-                out=y_rows[:, rows, h * HALF + cols.start : h * HALF + cols.stop], in_=y[h][:, rows, cols]
-            )
+        def store_unit(c, tiles):
+            nc.sync.dma_start(out=y_rows[:, tiles, c * QC : (c + 1) * QC], in_=y_part(c, tiles))
 
-        low, high, every = (0, 1), (2, 3), (0, 1, 2, 3)
-        for c in range(CHUNKS):
-            weave(nc.scalar.copy, q_bf[c][:], q_raw[c][:])
-        quantize_q(0, codes_at)
-        k_words = placed([P, N], U32, "k_words", raw_at[0])
+        for c in range(LAST):
+            weave_q(nc.scalar.copy, c, q_raw[c][:], 3 + c)
+        quantize_q(0, 6, 2048)
+        k_words = placed([P, N], U32, "k_words", 0)
         for r in range(PACK):
-            quantize(k_words[:, r * P : (r + 1) * P], k_scales[r][:], k_bf[:, r * P * PACK : (r + 1) * P * PACK])
-        quantize_q(1, codes_at + RAW)
-        banks = [scores((0,), low), scores((0,), high), scores((1,), every)]
-        weights(banks[0], (0,), low, keep.tile([P, PAIR, QC], F32, name="shifted0"))
-        quantize_q(2, codes_at + 2 * RAW)
-        bank2 = [scores((2,), low), scores((2,), high)]
-        weights(banks[1], (0,), high, placed([P, PAIR, QC], F32, "shifted1", raw_at[2] - RAW // 4))
-        store_y(0, slice(0, PACK), slice(0, QC))
-        weights(banks[2], (1,), every, placed([P, PACK, QC], F32, "shifted2", raw_at[2] + RAW // 2))
-        store_y(0, slice(0, PACK), slice(QC, HALF))
-        quantize_q(LAST, codes_at + RAW)
-        last = [scores((LAST,), low), scores((LAST,), high)]
-        for pair, tiles in enumerate((low, high)):
-            weights(bank2[pair], (2,), tiles, placed([P, PAIR, QC], F32, f"shifted3_{pair}", raw_at[LAST] + pair * RAW // 2))
-        for pair, tiles in enumerate((low, high)):
-            weights(last[pair], (LAST,), tiles, keep.tile([P, PAIR, QC], F32, name=f"shifted4_{pair}"))
-            store_y(1, slice(PAIR * pair, PAIR * (pair + 1)), slice(0, HALF))
+            quantize(k_words[:, r * P : (r + 1) * P], k_scales[r][:], k_bf[:, r])
+        scores(0)
+        quantize_q(1, 7, 2048)
+        scores(1)
+        weights(0, 0, 8, 2048)
+        store_unit(0, LOW)
+        quantize_q(2, 6, 2048 + 256)
+        scores(2)
+        weights(0, 1, 9, 2048)
+        store_unit(0, HIGH)
+        weave_q(nc.vector.tensor_copy, LAST, q_raw[LAST][:], 6, 2048 - 1024 + 256)
+        weights(1, 0, 18)
+        store_unit(1, LOW)
+        quantize_q(LAST, 7, 2048 + 256)
+        scores(LAST)
+        weights(1, 1, 19)
+        store_unit(1, HIGH)
+        for pair, tiles in enumerate((LOW, HIGH)):
+            weights(2, pair, 10 + pair)
+            weights(LAST, pair, 12 + pair)
+            nc.sync.dma_start(out=y_rows[:, tiles, HALF:], in_=y[1][:, tiles, :])
 
+        every = slice(0, PACK)
         y_codes = keep.tile([P, NQ], U32, name="y_codes", align_bytes=64)
         y_scales = keep.tile([P, NQ], U8, name="y_scales", align_bytes=64)
-        y_bf0 = placed([P, QC, PACK], BF16, "y_bf0", bf_at + LAST * RAW)
-        y_bf = placed([P, LAST * QC, PACK], BF16, "y_bf", codes_at + RAW + 64)
+        y_bf0 = placed([P, QC, PACK], BF16, "y_bf0", 6, 512)
+        y_bf1 = placed([P, QC, PACK], BF16, "y_bf1", 7, 2048 + 512)
+        y_bf2 = placed([P, QC, PACK], BF16, "y_bf2", 14)
+        y_bf3 = placed([P, QC, PACK], BF16, "y_bf3", 15)
+        y_bf = [y_bf0, y_bf1, y_bf2, y_bf3]
         word_rows = out_1[0].rearrange("p q t -> p (q t)").bitcast(I32)
-        nc.gpsimd.tensor_scalar(
-            out=y_bf0[:], in0=y[0][:, :, 0:QC].rearrange("p t c -> p c t"), scalar1=1.0, scalar2=0.0, op0=MULT, op1=ADD
-        )
 
         def quantize_y(c):
-            values = y_bf[:, (c - 1) * QC : c * QC, :] if c else y_bf0[:]
             cols = slice(c * QC, (c + 1) * QC)
-            quantize(y_codes[:, cols], y_scales[:, cols], values.rearrange("p c t -> p (c t)"))
+            quantize(y_codes[:, cols], y_scales[:, cols], y_bf[c][:])
 
-        weave(nc.vector.tensor_copy, y_bf[:, 0:QC, :], y[0][:, :, QC:])
-        weave(nc.vector.tensor_copy, y_bf[:, QC : 2 * QC, :], y[1][:, :, 0:QC])
+        share = 64
+        gpsimd_copy(y_bf0[:], y_part(0, every).rearrange("p t c -> p c t"))
+        gpsimd_copy(y_bf1[:, 0:share, :], y[0][:, :, QC : QC + share].rearrange("p t c -> p c t"))
+        weave(nc.vector.tensor_copy, y_bf1[:, share:, :], y[0][:, :, QC + share :])
         quantize_y(0)
+        weave(nc.vector.tensor_copy, y_bf2[:], y_part(2, every))
         quantize_y(1)
         nc.scalar.dma_start(out=word_rows[:, 0:HALF], in_=y_codes[:, 0:HALF].bitcast(I32))
-        split = 64
-        weave(nc.vector.tensor_copy, y_bf[:, 2 * QC : 2 * QC + split, :], y[1][:, :, QC : QC + split])
-        weave(nc.scalar.copy, y_bf[:, 2 * QC + split :, :], y[1][:, :, QC + split :])
+        split = 48
+        weave(nc.vector.tensor_copy, y_bf3[:, 0:split, :], y[1][:, :, QC : QC + split])
+        weave(nc.scalar.copy, y_bf3[:, split:, :], y[1][:, :, QC + split :])
         quantize_y(2)
         quantize_y(LAST)
         nc.sync.dma_start(out=word_rows[:, HALF:], in_=y_codes[:, HALF:].bitcast(I32))

@@ -175,15 +175,13 @@ def tile_attend_plw_softf_f_topk_kernel(tc, qT, kT, ls, offs, out_0, out_1, out_
             cols = slice(c * QC, (c + 1) * QC)
             quantize(y_codes[:, cols], y_scales[:, cols], y_bf[c][:])
 
-        share = 64
         gpsimd_copy(y_bf0[:], y_part(0, every).rearrange("p t c -> p c t"))
-        gpsimd_copy(y_bf1[:, 0:share, :], y[0][:, :, QC : QC + share].rearrange("p t c -> p c t"))
-        weave(nc.vector.tensor_copy, y_bf1[:, share:, :], y[0][:, :, QC + share :])
+        weave(nc.vector.tensor_copy, y_bf1[:], y_part(1, every))
         quantize_y(0)
         weave(nc.vector.tensor_copy, y_bf2[:], y_part(2, every))
         quantize_y(1)
         nc.scalar.dma_start(out=word_rows[:, 0:HALF], in_=y_codes[:, 0:HALF].bitcast(I32))
-        split = 48
+        split = 32
         weave(nc.vector.tensor_copy, y_bf3[:, 0:split, :], y[1][:, :, QC : QC + split])
         weave(nc.scalar.copy, y_bf3[:, split:, :], y[1][:, :, QC + split :])
         quantize_y(2)

@@ -29,7 +29,8 @@ LAST = CHUNKS - 1
 HALF = NQ // 2
 PAIR = 2
 ROOM = 8192
-LOW, HIGH = slice(0, PAIR), slice(PAIR, PACK)
+LOW, HIGH, EVERY = slice(0, PAIR), slice(PAIR, PACK), slice(0, PACK)
+UNITS = ((slice(0, 1), slice(1, PAIR), HIGH), (LOW, HIGH), (EVERY,), (LOW, HIGH))
 
 
 def weave(copy, dst, src):
@@ -47,6 +48,9 @@ def tile_attend_plw_softf_f_topk_kernel(tc, qT, kT, ls, offs, out_0, out_1, out_
 
     def gpsimd_copy(out, in_):
         nc.gpsimd.tensor_scalar(out=out, in0=in_, scalar1=1.0, scalar2=0.0, op0=MULT, op1=ADD)
+
+    def exp_to(out, in_):
+        nc.scalar.activation(out=out, in_=in_, func=EXP)
 
     with ExitStack() as ctx:
         keep = ctx.enter_context(tc.tile_pool(name="keep", bufs=1))
@@ -102,9 +106,10 @@ def tile_attend_plw_softf_f_topk_kernel(tc, qT, kT, ls, offs, out_0, out_1, out_
             quantize(q_codes[c][:], q_scales[c][:], q_bf[c][:])
 
         def scores(c):
-            for pair, tiles in enumerate((LOW, HIGH)):
-                u = PAIR * c + pair
-                banks[u] = psum.tile([P, PAIR, QC], F32, name=f"scores{u}", tag=f"bank{u}")
+            for tiles in UNITS[c]:
+                u = (c, tiles.start)
+                tag = f"bank{len(banks)}"
+                banks[u] = psum.tile([P, tiles.stop - tiles.start, QC], F32, name=f"scores{c}_{tiles.start}", tag=tag)
                 for r in range(tiles.start, tiles.stop):
                     nc.tensor.matmul_mx(
                         out=banks[u][:, r - tiles.start, :],
@@ -120,16 +125,17 @@ def tile_attend_plw_softf_f_topk_kernel(tc, qT, kT, ls, offs, out_0, out_1, out_
             h, lo = divmod(c * QC, HALF)
             return y[h][:, tiles, lo : lo + QC]
 
-        def weights(c, pair, room, byte=0):
-            u = PAIR * c + pair
-            shifted = placed([P, PAIR, QC], F32, f"shifted{u}", room, byte)
+        shifted = [keep.tile([P, PACK, QC], F32, name=f"shifted{c}") for c in range(CHUNKS)]
+
+        def weights(c, tiles):
+            u = (c, tiles.start)
             nc.vector.tensor_tensor(
-                out=shifted[:],
+                out=shifted[c][:, tiles, :],
                 in0=banks[u][:],
-                in1=ls_all[:, c * QC : (c + 1) * QC].unsqueeze(1).to_broadcast([P, PAIR, QC]),
+                in1=ls_all[:, c * QC : (c + 1) * QC].unsqueeze(1).to_broadcast([P, tiles.stop - tiles.start, QC]),
                 op=SUB,
             )
-            nc.scalar.activation(out=y_part(c, (LOW, HIGH)[pair]), in_=shifted[:], func=EXP)
+            nc.scalar.activation(out=y_part(c, tiles), in_=shifted[c][:, tiles, :], func=EXP)
 
         def store_unit(c, tiles):
             nc.sync.dma_start(out=y_rows[:, tiles, c * QC : (c + 1) * QC], in_=y_part(c, tiles))
@@ -143,25 +149,23 @@ def tile_attend_plw_softf_f_topk_kernel(tc, qT, kT, ls, offs, out_0, out_1, out_
         scores(0)
         quantize_q(1, 7, 2048)
         scores(1)
-        weights(0, 0, 8, 2048)
-        store_unit(0, LOW)
+        weights(0, UNITS[0][0])
+        weights(0, UNITS[0][1])
         quantize_q(2, 6, 2048 + 256)
         scores(2)
-        weights(0, 1, 9, 2048)
-        store_unit(0, HIGH)
+        weights(0, HIGH)
+        store_unit(0, EVERY)
         weave_q(nc.vector.tensor_copy, LAST, q_raw[LAST][:], 6, 2048 - 1024 + 256)
-        weights(1, 0, 18)
-        store_unit(1, LOW)
+        weights(1, LOW)
         quantize_q(LAST, 7, 2048 + 256)
         scores(LAST)
-        weights(1, 1, 19)
-        store_unit(1, HIGH)
-        for pair, tiles in enumerate((LOW, HIGH)):
-            weights(2, pair, 10 + pair)
-            weights(LAST, pair, 12 + pair)
+        weights(1, HIGH)
+        store_unit(1, EVERY)
+        weights(2, EVERY)
+        for tiles in (LOW, HIGH):
+            weights(LAST, tiles)
             nc.sync.dma_start(out=y_rows[:, tiles, HALF:], in_=y[1][:, tiles, :])
 
-        every = slice(0, PACK)
         y_codes = keep.tile([P, NQ], U32, name="y_codes", align_bytes=64)
         y_scales = keep.tile([P, NQ], U8, name="y_scales", align_bytes=64)
         y_bf0 = placed([P, QC, PACK], BF16, "y_bf0", 6, 512)
@@ -175,15 +179,13 @@ def tile_attend_plw_softf_f_topk_kernel(tc, qT, kT, ls, offs, out_0, out_1, out_
             cols = slice(c * QC, (c + 1) * QC)
             quantize(y_codes[:, cols], y_scales[:, cols], y_bf[c][:])
 
-        gpsimd_copy(y_bf0[:], y_part(0, every).rearrange("p t c -> p c t"))
-        weave(nc.vector.tensor_copy, y_bf1[:], y_part(1, every))
+        gpsimd_copy(y_bf0[:], y_part(0, EVERY).rearrange("p t c -> p c t"))
+        weave(nc.vector.tensor_copy, y_bf1[:], y_part(1, EVERY))
+        weave(nc.vector.tensor_copy, y_bf2[:], y_part(2, EVERY))
+        weave(exp_to, y_bf3[:], shifted[LAST][:])
         quantize_y(0)
-        weave(nc.vector.tensor_copy, y_bf2[:], y_part(2, every))
         quantize_y(1)
         nc.scalar.dma_start(out=word_rows[:, 0:HALF], in_=y_codes[:, 0:HALF].bitcast(I32))
-        split = 32
-        weave(nc.vector.tensor_copy, y_bf3[:, 0:split, :], y[1][:, :, QC : QC + split])
-        weave(nc.scalar.copy, y_bf3[:, split:, :], y[1][:, :, QC + split :])
         quantize_y(2)
         quantize_y(LAST)
         nc.sync.dma_start(out=word_rows[:, HALF:], in_=y_codes[:, HALF:].bitcast(I32))

@@ -30,7 +30,8 @@ HALF = NQ // 2
 PAIR = 2
 ROOM = 8192
 LOW, HIGH, EVERY = slice(0, PAIR), slice(PAIR, PACK), slice(0, PACK)
-UNITS = ((slice(0, 1), slice(1, PAIR), HIGH), (LOW, HIGH), (EVERY,), (LOW, HIGH))
+UNITS = ((slice(0, 1), slice(1, PAIR), HIGH), (LOW, HIGH), (LOW, HIGH), (LOW, HIGH))
+BANKS = 8
 
 
 def weave(copy, dst, src):
@@ -108,7 +109,7 @@ def tile_attend_plw_softf_f_topk_kernel(tc, qT, kT, ls, offs, out_0, out_1, out_
         def scores(c):
             for tiles in UNITS[c]:
                 u = (c, tiles.start)
-                tag = f"bank{len(banks)}"
+                tag = f"bank{len(banks) % BANKS}"
                 banks[u] = psum.tile([P, tiles.stop - tiles.start, QC], F32, name=f"scores{c}_{tiles.start}", tag=tag)
                 for r in range(tiles.start, tiles.stop):
                     nc.tensor.matmul_mx(
@@ -140,8 +141,8 @@ def tile_attend_plw_softf_f_topk_kernel(tc, qT, kT, ls, offs, out_0, out_1, out_
         def store_unit(c, tiles):
             nc.sync.dma_start(out=y_rows[:, tiles, c * QC : (c + 1) * QC], in_=y_part(c, tiles))
 
-        for c in range(LAST):
-            weave_q(nc.scalar.copy, c, q_raw[c][:], 3 + c)
+        for c in range(CHUNKS):
+            weave_q(nc.scalar.copy, c, q_raw[c][:], (3, 4, 5, 10)[c])
         quantize_q(0, 6, 2048)
         k_words = placed([P, N], U32, "k_words", 0)
         for r in range(PACK):
@@ -155,20 +156,20 @@ def tile_attend_plw_softf_f_topk_kernel(tc, qT, kT, ls, offs, out_0, out_1, out_
         scores(2)
         weights(0, HIGH)
         store_unit(0, EVERY)
-        weave_q(nc.vector.tensor_copy, LAST, q_raw[LAST][:], 6, 2048 - 1024 + 256)
         weights(1, LOW)
-        quantize_q(LAST, 7, 2048 + 256)
-        scores(LAST)
         weights(1, HIGH)
         store_unit(1, EVERY)
-        weights(2, EVERY)
+        quantize_q(LAST, 7, 2048 + 256)
+        scores(LAST)
+        weights(2, LOW)
+        weights(2, HIGH)
         for tiles in (LOW, HIGH):
             weights(LAST, tiles)
             nc.sync.dma_start(out=y_rows[:, tiles, HALF:], in_=y[1][:, tiles, :])
 
         y_codes = keep.tile([P, NQ], U32, name="y_codes", align_bytes=64)
         y_scales = keep.tile([P, NQ], U8, name="y_scales", align_bytes=64)
-        y_bf0 = placed([P, QC, PACK], BF16, "y_bf0", 6, 512)
+        y_bf0 = placed([P, QC, PACK], BF16, "y_bf0", 10)
         y_bf1 = placed([P, QC, PACK], BF16, "y_bf1", 7, 2048 + 512)
         y_bf2 = placed([P, QC, PACK], BF16, "y_bf2", 14)
         y_bf3 = placed([P, QC, PACK], BF16, "y_bf3", 15)

@@ -34,10 +34,10 @@ UNITS = ((slice(0, 1), slice(1, PAIR), HIGH), (LOW, HIGH), (LOW, HIGH), (LOW, HI
 BANKS = 8
 
 
-def weave(copy, dst, src):
+def weave(copy, dst, src, run=PACK):
     copy(
-        out=dst.rearrange("p (c i) t -> p c t i", i=PACK),
-        in_=src.rearrange("p t (c i) -> p c t i", i=PACK),
+        out=dst.rearrange("p (c i) t -> p c t i", i=run),
+        in_=src.rearrange("p t (c i) -> p c t i", i=run),
     )
 
 
@@ -100,7 +100,7 @@ def tile_attend_plw_softf_f_topk_kernel(tc, qT, kT, ls, offs, out_0, out_1, out_
 
         def weave_q(copy, c, src, room, byte=0):
             q_bf[c] = placed([P, QC, PACK], BF16, f"q_bf{c}", room, byte)
-            weave(copy, q_bf[c][:], src)
+            weave(copy, q_bf[c][:], src, PAIR)
 
         def quantize_q(c, room, byte=0):
             q_codes[c] = placed([P, QC], U32, f"q_codes{c}", room, byte)
@@ -152,10 +152,10 @@ def tile_attend_plw_softf_f_topk_kernel(tc, qT, kT, ls, offs, out_0, out_1, out_
         scores(1)
         weights(0, UNITS[0][0])
         weights(0, UNITS[0][1])
-        quantize_q(2, 6, 2048 + 256)
-        scores(2)
         weights(0, HIGH)
         store_unit(0, EVERY)
+        quantize_q(2, 6, 2048 + 256)
+        scores(2)
         weights(1, LOW)
         weights(1, HIGH)
         store_unit(1, EVERY)

@@ -32,6 +32,7 @@ ROOM = 8192
 LOW, HIGH, EVERY = slice(0, PAIR), slice(PAIR, PACK), slice(0, PACK)
 UNITS = ((slice(0, 1), slice(1, PAIR), HIGH), (LOW, HIGH), (LOW, HIGH), (LOW, HIGH))
 BANKS = 8
+SHARE = 64
 
 
 def weave(copy, dst, src, run=PACK):
@@ -128,21 +129,22 @@ def tile_attend_plw_softf_f_topk_kernel(tc, qT, kT, ls, offs, out_0, out_1, out_
 
         shifted = [keep.tile([P, PACK, QC], F32, name=f"shifted{c}") for c in range(CHUNKS)]
 
-        def weights(c, tiles):
+        def weights(c, tiles, held=None):
             u = (c, tiles.start)
+            diff = shifted[c][:, tiles, :] if held is None else held[:]
             nc.vector.tensor_tensor(
-                out=shifted[c][:, tiles, :],
+                out=diff,
                 in0=banks[u][:],
                 in1=ls_all[:, c * QC : (c + 1) * QC].unsqueeze(1).to_broadcast([P, tiles.stop - tiles.start, QC]),
                 op=SUB,
             )
-            nc.scalar.activation(out=y_part(c, tiles), in_=shifted[c][:, tiles, :], func=EXP)
+            nc.scalar.activation(out=y_part(c, tiles), in_=diff, func=EXP)
 
         def store_unit(c, tiles):
             nc.sync.dma_start(out=y_rows[:, tiles, c * QC : (c + 1) * QC], in_=y_part(c, tiles))
 
-        for c in range(CHUNKS):
-            weave_q(nc.scalar.copy, c, q_raw[c][:], (3, 4, 5, 10)[c])
+        for c in range(LAST):
+            weave_q(nc.scalar.copy, c, q_raw[c][:], 3 + c)
         quantize_q(0, 6, 2048)
         k_words = placed([P, N], U32, "k_words", 0)
         for r in range(PACK):
@@ -150,17 +152,20 @@ def tile_attend_plw_softf_f_topk_kernel(tc, qT, kT, ls, offs, out_0, out_1, out_
         scores(0)
         quantize_q(1, 7, 2048)
         scores(1)
+        q_bf[LAST] = placed([P, QC, PACK], BF16, "q_bf3", 6, 2048 - 1024 + 256)
+        weave(nc.scalar.copy, q_bf[LAST][:, SHARE:, :], q_raw[LAST][:, :, SHARE:], PAIR)
         weights(0, UNITS[0][0])
         weights(0, UNITS[0][1])
         weights(0, HIGH)
         store_unit(0, EVERY)
         quantize_q(2, 6, 2048 + 256)
         scores(2)
+        weave(nc.vector.tensor_copy, q_bf[LAST][:, 0:SHARE, :], q_raw[LAST][:, :, 0:SHARE])
         weights(1, LOW)
-        weights(1, HIGH)
-        store_unit(1, EVERY)
         quantize_q(LAST, 7, 2048 + 256)
         scores(LAST)
+        weights(1, HIGH, placed([P, PAIR, QC], F32, "held", 2))
+        store_unit(1, EVERY)
         weights(2, LOW)
         weights(2, HIGH)
         for tiles in (LOW, HIGH):
@@ -169,7 +174,7 @@ def tile_attend_plw_softf_f_topk_kernel(tc, qT, kT, ls, offs, out_0, out_1, out_
 
         y_codes = keep.tile([P, NQ], U32, name="y_codes", align_bytes=64)
         y_scales = keep.tile([P, NQ], U8, name="y_scales", align_bytes=64)
-        y_bf0 = placed([P, QC, PACK], BF16, "y_bf0", 10)
+        y_bf0 = placed([P, QC, PACK], BF16, "y_bf0", 6, 512)
         y_bf1 = placed([P, QC, PACK], BF16, "y_bf1", 7, 2048 + 512)
         y_bf2 = placed([P, QC, PACK], BF16, "y_bf2", 14)
         y_bf3 = placed([P, QC, PACK], BF16, "y_bf3", 15)

@@ -30,9 +30,9 @@ HALF = NQ // 2
 PAIR = 2
 ROOM = 8192
 LOW, HIGH, EVERY = slice(0, PAIR), slice(PAIR, PACK), slice(0, PACK)
-UNITS = ((slice(0, 1), slice(1, PAIR), HIGH), (LOW, HIGH), (LOW, HIGH), (LOW, HIGH))
+UNITS = (tuple(slice(r, r + 1) for r in range(PACK)), (LOW, HIGH), (LOW, HIGH), (LOW, HIGH))
 BANKS = 8
-SHARE = 64
+SHARE = 48
 
 
 def weave(copy, dst, src, run=PACK):
@@ -154,9 +154,8 @@ def tile_attend_plw_softf_f_topk_kernel(tc, qT, kT, ls, offs, out_0, out_1, out_
         scores(1)
         q_bf[LAST] = placed([P, QC, PACK], BF16, "q_bf3", 6, 2048 - 1024 + 256)
         weave(nc.scalar.copy, q_bf[LAST][:, SHARE:, :], q_raw[LAST][:, :, SHARE:], PAIR)
-        weights(0, UNITS[0][0])
-        weights(0, UNITS[0][1])
-        weights(0, HIGH)
+        for tiles in UNITS[0]:
+            weights(0, tiles)
         store_unit(0, EVERY)
         quantize_q(2, 6, 2048 + 256)
         scores(2)
@@ -188,10 +187,12 @@ def tile_attend_plw_softf_f_topk_kernel(tc, qT, kT, ls, offs, out_0, out_1, out_
         gpsimd_copy(y_bf0[:], y_part(0, EVERY).rearrange("p t c -> p c t"))
         weave(nc.vector.tensor_copy, y_bf1[:], y_part(1, EVERY))
         weave(nc.vector.tensor_copy, y_bf2[:], y_part(2, EVERY))
-        weave(exp_to, y_bf3[:], shifted[LAST][:])
+        split = 32
+        weave(exp_to, y_bf3[:, split:, :], shifted[LAST][:, :, split:])
         quantize_y(0)
         quantize_y(1)
         nc.scalar.dma_start(out=word_rows[:, 0:HALF], in_=y_codes[:, 0:HALF].bitcast(I32))
+        weave(nc.vector.tensor_copy, y_bf3[:, 0:split, :], y[1][:, :, QC : QC + split])
         quantize_y(2)
         quantize_y(LAST)
         nc.sync.dma_start(out=word_rows[:, HALF:], in_=y_codes[:, HALF:].bitcast(I32))

@@ -60,11 +60,11 @@ def tile_attend_plw_softf_f_topk_kernel(tc, qT, kT, ls, offs, out_0, out_1, out_
         psum = ctx.enter_context(tc.psum_pool(name="psum", bufs=1))
 
         def placed(shape, dtype, name, room, byte=0):
-            return reuse.tile(shape, dtype, name=name, offset=room * ROOM + byte, align_bytes=64)
+            return reuse.tile(shape, dtype, name=name, offset=room * ROOM + byte, align_bytes=256)
 
         offsets = keep.tile([P, N // LIST_ROWS], U16, name="offsets")
         ls_col = keep.tile([P, PACK], F32, name="ls_col")
-        planes = [keep.tile([P, T], F32, name=f"plane{t}") for t in range(PACK)]
+        planes = [keep.tile([P, T], F32, name=f"plane{t}", align_bytes=256) for t in range(PACK)]
         q_raw = [placed([P, PACK, QC], F32, f"q_raw{c}", (0, 1, 16, 2)[c]) for c in range(CHUNKS)]
         k_rows = kT.rearrange("(p t) n -> t p n", t=PACK)
         q_rows = qT[0].rearrange("(p t) n -> p t n", t=PACK)
@@ -76,27 +76,27 @@ def tile_attend_plw_softf_f_topk_kernel(tc, qT, kT, ls, offs, out_0, out_1, out_
         for c in range(CHUNKS):
             nc.sync.dma_start(out=q_raw[c][:], in_=q_rows[:, :, c * QC : (c + 1) * QC])
 
-        ident = keep.tile([P, P], F32, name="ident")
+        ident = keep.tile([P, P], F32, name="ident", align_bytes=256)
         make_identity(nc, ident[:])
         ls_ps = psum.tile([P, PACK, P], F32, name="ls_ps", tag="bank7")
         for c in range(PACK):
             nc.tensor.transpose(ls_ps[:, c, :], ls_col[:, c : c + 1].to_broadcast([P, P]), ident[:])
-        ls_all = keep.tile([P, NQ], F32, name="ls_all")
+        ls_all = keep.tile([P, NQ], F32, name="ls_all", align_bytes=256)
         nc.scalar.activation(
             out=ls_all[:].rearrange("p (n c) -> p n c", c=PACK),
             in_=ls_ps[:].rearrange("p c n -> p n c"),
             func=COPY,
         )
 
-        k_bf = keep.tile([P, PACK, P, PACK], BF16, name="k_bf", align_bytes=64)
+        k_bf = keep.tile([P, PACK, P, PACK], BF16, name="k_bf", align_bytes=256)
         k_dealt = k_bf[:].rearrange("p r s t -> p s r t")
         for t in range(PACK):
             nc.vector.tensor_copy(out=k_dealt[:, :, :, t], in_=planes[t][:].indirect(offsets[:]))
 
-        q_scales = [keep.tile([P, QC], U8, name=f"q_scales{c}", align_bytes=64) for c in range(CHUNKS)]
-        k_scales = [keep.tile([P, P], U8, name=f"k_scales{r}", align_bytes=64) for r in range(PACK)]
+        q_scales = [keep.tile([P, QC], U8, name=f"q_scales{c}", align_bytes=256) for c in range(CHUNKS)]
+        k_scales = [keep.tile([P, P], U8, name=f"k_scales{r}", align_bytes=256) for r in range(PACK)]
         y_rows = out_0.rearrange("(p r) q -> p r q", r=PACK)
-        y = [keep.tile([P, PACK, HALF], F32, name=f"y{h}") for h in range(NQ // HALF)]
+        y = [keep.tile([P, PACK, HALF], F32, name=f"y{h}", align_bytes=256) for h in range(NQ // HALF)]
         q_bf, q_codes, banks = {}, {}, {}
 
         def weave_q(copy, c, src, room, byte=0):
@@ -127,7 +127,7 @@ def tile_attend_plw_softf_f_topk_kernel(tc, qT, kT, ls, offs, out_0, out_1, out_
             h, lo = divmod(c * QC, HALF)
             return y[h][:, tiles, lo : lo + QC]
 
-        shifted = [keep.tile([P, PACK, QC], F32, name=f"shifted{c}") for c in range(CHUNKS)]
+        shifted = [keep.tile([P, PACK, QC], F32, name=f"shifted{c}", align_bytes=256) for c in range(CHUNKS)]
 
         def weights(c, tiles, held=None):
             u = (c, tiles.start)
@@ -171,8 +171,8 @@ def tile_attend_plw_softf_f_topk_kernel(tc, qT, kT, ls, offs, out_0, out_1, out_
             weights(LAST, tiles)
             nc.sync.dma_start(out=y_rows[:, tiles, HALF:], in_=y[1][:, tiles, :])
 
-        y_codes = keep.tile([P, NQ], U32, name="y_codes", align_bytes=64)
-        y_scales = keep.tile([P, NQ], U8, name="y_scales", align_bytes=64)
+        y_codes = keep.tile([P, NQ], U32, name="y_codes", align_bytes=256)
+        y_scales = keep.tile([P, NQ], U8, name="y_scales", align_bytes=256)
         y_bf0 = placed([P, QC, PACK], BF16, "y_bf0", 6, 512)
         y_bf1 = placed([P, QC, PACK], BF16, "y_bf1", 7, 2048 + 512)
         y_bf2 = placed([P, QC, PACK], BF16, "y_bf2", 14)

@@ -82,11 +82,10 @@ def tile_attend_plw_softf_f_topk_kernel(tc, qT, kT, ls, offs, out_0, out_1, out_
         for c in range(PACK):
             nc.tensor.transpose(ls_ps[:, c, :], ls_col[:, c : c + 1].to_broadcast([P, P]), ident[:])
         ls_all = keep.tile([P, NQ], F32, name="ls_all", align_bytes=256)
-        nc.scalar.activation(
-            out=ls_all[:].rearrange("p (n c) -> p n c", c=PACK),
-            in_=ls_ps[:].rearrange("p c n -> p n c"),
-            func=COPY,
-        )
+        ls_out = ls_all[:].rearrange("p (n c) -> p n c", c=PACK)
+        ls_in = ls_ps[:].rearrange("p c n -> p n c")
+        nc.scalar.copy(out=ls_out[:, 0 : P // 2, :], in_=ls_in[:, 0 : P // 2, :])
+        nc.scalar.activation(out=ls_out[:, P // 2 :, :], in_=ls_in[:, P // 2 :, :], func=COPY)
 
         k_bf = keep.tile([P, PACK, P, PACK], BF16, name="k_bf", align_bytes=256)
         k_dealt = k_bf[:].rearrange("p r s t -> p s r t")

@@ -33,6 +33,8 @@ LOW, HIGH, EVERY = slice(0, PAIR), slice(PAIR, PACK), slice(0, PACK)
 UNITS = (tuple(slice(r, r + 1) for r in range(PACK)), (LOW, HIGH), (LOW, HIGH), (LOW, HIGH))
 BANKS = 8
 SHARE = 48
+LS_ROW = 8
+LS_ROWS = NQ // LS_ROW
 
 
 def weave(copy, dst, src, run=PACK):
@@ -63,14 +65,14 @@ def tile_attend_plw_softf_f_topk_kernel(tc, qT, kT, ls, offs, out_0, out_1, out_
             return reuse.tile(shape, dtype, name=name, offset=room * ROOM + byte, align_bytes=256)
 
         offsets = keep.tile([P, N // LIST_ROWS], U16, name="offsets")
-        ls_col = keep.tile([P, PACK], F32, name="ls_col")
+        ls_col = keep.tile([P, LS_ROW], F32, name="ls_col")
         planes = [keep.tile([P, T], F32, name=f"plane{t}", align_bytes=256) for t in range(PACK)]
         q_raw = [placed([P, PACK, QC], F32, f"q_raw{c}", (0, 1, 16, 2)[c]) for c in range(CHUNKS)]
         k_rows = kT.rearrange("(p t) n -> t p n", t=PACK)
         q_rows = qT[0].rearrange("(p t) n -> p t n", t=PACK)
         nc.sync.dma_start(out=planes[0][:], in_=k_rows[0])
         nc.sync.dma_start(offsets[:], offs)
-        nc.scalar.dma_start(out=ls_col[:], in_=ls[0, 0].rearrange("(p c) -> p c", c=PACK))
+        nc.scalar.dma_start(out=ls_col[0:LS_ROWS, :], in_=ls[0, 0].rearrange("(p c) -> p c", c=LS_ROW))
         for t in range(1, PACK):
             nc.sync.dma_start(out=planes[t][:], in_=k_rows[t])
         for c in range(CHUNKS):
@@ -78,14 +80,19 @@ def tile_attend_plw_softf_f_topk_kernel(tc, qT, kT, ls, offs, out_0, out_1, out_
 
         ident = keep.tile([P, P], F32, name="ident", align_bytes=256)
         make_identity(nc, ident[:])
-        ls_ps = psum.tile([P, PACK, P], F32, name="ls_ps", tag="bank7")
-        for c in range(PACK):
-            nc.tensor.transpose(ls_ps[:, c, :], ls_col[:, c : c + 1].to_broadcast([P, P]), ident[:])
+        nc.gpsimd.memset(ls_col[LS_ROWS:, :], 0.0)
         ls_all = keep.tile([P, NQ], F32, name="ls_all", align_bytes=256)
-        ls_out = ls_all[:].rearrange("p (n c) -> p n c", c=PACK)
-        ls_in = ls_ps[:].rearrange("p c n -> p n c")
-        nc.scalar.copy(out=ls_out[:, 0 : P // 2, :], in_=ls_in[:, 0 : P // 2, :])
-        nc.scalar.activation(out=ls_out[:, P // 2 :, :], in_=ls_in[:, P // 2 :, :], func=COPY)
+        ls_out = ls_all[:].rearrange("p (n c) -> p n c", c=LS_ROW)
+        for g in range(LS_ROW // PACK):
+            ls_ps = psum.tile([P, PACK, P], F32, name=f"ls_ps{g}", tag=f"bank{BANKS - 1 - g}")
+            for c in range(PACK):
+                col = g * PACK + c
+                nc.tensor.transpose(ls_ps[:, c, :], ls_col[:, col : col + 1].to_broadcast([P, P]), ident[:])
+            nc.scalar.activation(
+                out=ls_out[:, :, g * PACK : (g + 1) * PACK],
+                in_=ls_ps[:, :, 0:LS_ROWS].rearrange("p c n -> p n c"),
+                func=COPY,
+            )
 
         k_bf = keep.tile([P, PACK, P, PACK], BF16, name="k_bf", align_bytes=256)
         k_dealt = k_bf[:].rearrange("p r s t -> p s r t")

@@ -33,6 +33,7 @@ LOW, HIGH, EVERY = slice(0, PAIR), slice(PAIR, PACK), slice(0, PACK)
 UNITS = (tuple(slice(r, r + 1) for r in range(PACK)), (LOW, HIGH), (LOW, HIGH), (LOW, HIGH))
 BANKS = 8
 SHARE = 48
+GATHER_V = 256
 LS_ROW = 8
 LS_ROWS = NQ // LS_ROW
 
@@ -96,8 +97,16 @@ def tile_attend_plw_softf_f_topk_kernel(tc, qT, kT, ls, offs, out_0, out_1, out_
 
         k_bf = keep.tile([P, PACK, P, PACK], BF16, name="k_bf", align_bytes=256)
         k_dealt = k_bf[:].rearrange("p r s t -> p s r t")
-        for t in range(PACK):
+        for t in range(PACK - 1):
             nc.vector.tensor_copy(out=k_dealt[:, :, :, t], in_=planes[t][:].indirect(offsets[:]))
+        last = planes[PACK - 1]
+        rows_v, cols_v = GATHER_V // PACK, GATHER_V // LIST_ROWS
+        k_tail = keep.tile([P, N - GATHER_V], BF16, name="k_tail", align_bytes=256)
+        nc.vector.tensor_copy(out=k_dealt[:, 0:rows_v, :, PACK - 1], in_=last[:].indirect(offsets[:, 0:cols_v]))
+        nc.scalar.activation(out=k_tail[:], in_=last[:].indirect(offsets[:, cols_v:]), func=COPY)
+        nc.vector.tensor_copy(
+            out=k_bf[:, :, rows_v:, PACK - 1], in_=k_tail[:].rearrange("p (s r) -> p r s", r=PACK)
+        )
 
         q_scales = [keep.tile([P, QC], U8, name=f"q_scales{c}", align_bytes=256) for c in range(CHUNKS)]
         k_scales = [keep.tile([P, P], U8, name=f"k_scales{r}", align_bytes=256) for r in range(PACK)]
@@ -121,7 +130,7 @@ def tile_attend_plw_softf_f_topk_kernel(tc, qT, kT, ls, offs, out_0, out_1, out_
                 for r in range(tiles.start, tiles.stop):
                     nc.tensor.matmul_mx(
                         out=banks[u][:, r - tiles.start, :],
-                        lhsT=k_words[:, r * P : (r + 1) * P].bitcast(FP8X4),
+                        lhsT=k_words[r][:].bitcast(FP8X4),
                         lhsT_scale=k_scales[r][:],
                         rhs=q_codes[c][:].bitcast(FP8X4),
                         rhs_scale=q_scales[c][:],
@@ -133,7 +142,7 @@ def tile_attend_plw_softf_f_topk_kernel(tc, qT, kT, ls, offs, out_0, out_1, out_
             h, lo = divmod(c * QC, HALF)
             return y[h][:, tiles, lo : lo + QC]
 
-        shifted = [keep.tile([P, PACK, QC], F32, name=f"shifted{c}", align_bytes=256) for c in range(CHUNKS)]
+        shifted = {c: keep.tile([P, PACK, QC], F32, name=f"shifted{c}", align_bytes=256) for c in range(1, CHUNKS)}
 
         def weights(c, tiles, held=None):
             u = (c, tiles.start)
@@ -151,15 +160,18 @@ def tile_attend_plw_softf_f_topk_kernel(tc, qT, kT, ls, offs, out_0, out_1, out_
 
         for c in range(LAST):
             weave_q(nc.scalar.copy, c, q_raw[c][:], 3 + c)
+        k_words = [keep.tile([P, P], U32, name="k_words0", align_bytes=256)]
+        quantize(k_words[0][:], k_scales[0][:], k_bf[:, 0])
         quantize_q(0, 6, 2048)
-        k_words = placed([P, N], U32, "k_words", 0)
-        for r in range(PACK):
-            quantize(k_words[:, r * P : (r + 1) * P], k_scales[r][:], k_bf[:, r])
+        for r in range(1, PACK):
+            k_words.append(placed([P, P], U32, f"k_words{r}", 0, r * 512))
+            quantize(k_words[r][:], k_scales[r][:], k_bf[:, r])
         scores(0)
         quantize_q(1, 7, 2048)
         scores(1)
         q_bf[LAST] = placed([P, QC, PACK], BF16, "q_bf3", 6, 2048 - 1024 + 256)
         weave(nc.scalar.copy, q_bf[LAST][:, SHARE:, :], q_raw[LAST][:, :, SHARE:], PAIR)
+        shifted[0] = placed([P, PACK, QC], F32, "shifted0", 1)
         for tiles in UNITS[0]:
             weights(0, tiles)
         store_unit(0, EVERY)

@@ -32,7 +32,8 @@ ROOM = 8192
 LOW, HIGH, EVERY = slice(0, PAIR), slice(PAIR, PACK), slice(0, PACK)
 UNITS = (tuple(slice(r, r + 1) for r in range(PACK)), (LOW, HIGH), (LOW, HIGH), (LOW, HIGH))
 BANKS = 8
-SHARE = 48
+SHARE = 32
+Q0_SHARE = 48
 GATHER_V = 256
 LS_ROW = 8
 LS_ROWS = NQ // LS_ROW
@@ -144,7 +145,7 @@ def tile_attend_plw_softf_f_topk_kernel(tc, qT, kT, ls, offs, out_0, out_1, out_
 
         shifted = {c: keep.tile([P, PACK, QC], F32, name=f"shifted{c}", align_bytes=256) for c in range(1, CHUNKS)}
 
-        def weights(c, tiles, held=None):
+        def weights(c, tiles, held=None, exp_tiles=None):
             u = (c, tiles.start)
             diff = shifted[c][:, tiles, :] if held is None else held[:]
             nc.vector.tensor_tensor(
@@ -153,12 +154,18 @@ def tile_attend_plw_softf_f_topk_kernel(tc, qT, kT, ls, offs, out_0, out_1, out_
                 in1=ls_all[:, c * QC : (c + 1) * QC].unsqueeze(1).to_broadcast([P, tiles.stop - tiles.start, QC]),
                 op=SUB,
             )
-            nc.scalar.activation(out=y_part(c, tiles), in_=diff, func=EXP)
+            if exp_tiles is None:
+                exp_to(y_part(c, tiles), diff)
+            elif tiles.stop == exp_tiles.stop:
+                exp_to(y_part(c, exp_tiles), shifted[c][:, exp_tiles, :])
 
         def store_unit(c, tiles):
             nc.sync.dma_start(out=y_rows[:, tiles, c * QC : (c + 1) * QC], in_=y_part(c, tiles))
 
-        for c in range(LAST):
+        q_bf[0] = placed([P, QC, PACK], BF16, "q_bf0", 3)
+        weave(nc.scalar.copy, q_bf[0][:, Q0_SHARE:, :], q_raw[0][:, :, Q0_SHARE:], PAIR)
+        weave(nc.vector.tensor_copy, q_bf[0][:, 0:Q0_SHARE, :], q_raw[0][:, :, 0:Q0_SHARE])
+        for c in range(1, LAST):
             weave_q(nc.scalar.copy, c, q_raw[c][:], 3 + c)
         k_words = [keep.tile([P, P], U32, name="k_words0", align_bytes=256)]
         quantize(k_words[0][:], k_scales[0][:], k_bf[:, 0])
@@ -173,7 +180,7 @@ def tile_attend_plw_softf_f_topk_kernel(tc, qT, kT, ls, offs, out_0, out_1, out_
         weave(nc.scalar.copy, q_bf[LAST][:, SHARE:, :], q_raw[LAST][:, :, SHARE:], PAIR)
         shifted[0] = placed([P, PACK, QC], F32, "shifted0", 1)
         for tiles in UNITS[0]:
-            weights(0, tiles)
+            weights(0, tiles, exp_tiles=LOW if tiles.start < PAIR else HIGH)
         store_unit(0, EVERY)
         quantize_q(2, 6, 2048 + 256)
         scores(2)

@@ -34,7 +34,7 @@ UNITS = (tuple(slice(r, r + 1) for r in range(PACK)), (LOW, HIGH), (LOW, HIGH), 
 BANKS = 8
 SHARE = 32
 Q0_SHARE = 48
-GATHER_V = 256
+GATHER_V = 288
 LS_ROW = 8
 LS_ROWS = NQ // LS_ROW
 

@@ -33,8 +33,7 @@ LOW, HIGH, EVERY = slice(0, PAIR), slice(PAIR, PACK), slice(0, PACK)
 UNITS = (tuple(slice(r, r + 1) for r in range(PACK)), (LOW, HIGH), (LOW, HIGH), (LOW, HIGH))
 BANKS = 8
 SHARE = 32
-Q0_SHARE = 48
-GATHER_V = 288
+GATHER_V = 320
 LS_ROW = 8
 LS_ROWS = NQ // LS_ROW
 
@@ -162,15 +161,11 @@ def tile_attend_plw_softf_f_topk_kernel(tc, qT, kT, ls, offs, out_0, out_1, out_
         def store_unit(c, tiles):
             nc.sync.dma_start(out=y_rows[:, tiles, c * QC : (c + 1) * QC], in_=y_part(c, tiles))
 
-        q_bf[0] = placed([P, QC, PACK], BF16, "q_bf0", 3)
-        weave(nc.scalar.copy, q_bf[0][:, Q0_SHARE:, :], q_raw[0][:, :, Q0_SHARE:], PAIR)
-        weave(nc.vector.tensor_copy, q_bf[0][:, 0:Q0_SHARE, :], q_raw[0][:, :, 0:Q0_SHARE])
-        for c in range(1, LAST):
+        for c in range(LAST):
             weave_q(nc.scalar.copy, c, q_raw[c][:], 3 + c)
-        k_words = [keep.tile([P, P], U32, name="k_words0", align_bytes=256)]
-        quantize(k_words[0][:], k_scales[0][:], k_bf[:, 0])
         quantize_q(0, 6, 2048)
-        for r in range(1, PACK):
+        k_words = []
+        for r in range(PACK):
             k_words.append(placed([P, P], U32, f"k_words{r}", 0, r * 512))
             quantize(k_words[r][:], k_scales[r][:], k_bf[:, r])
         scores(0)

@@ -33,7 +33,7 @@ LOW, HIGH, EVERY = slice(0, PAIR), slice(PAIR, PACK), slice(0, PACK)
 UNITS = (tuple(slice(r, r + 1) for r in range(PACK)), (LOW, HIGH), (LOW, HIGH), (LOW, HIGH))
 BANKS = 8
 SHARE = 32
-GATHER_V = 320
+GATHER_V = 288
 LS_ROW = 8
 LS_ROWS = NQ // LS_ROW
 
@@ -104,9 +104,9 @@ def tile_attend_plw_softf_f_topk_kernel(tc, qT, kT, ls, offs, out_0, out_1, out_
         k_tail = keep.tile([P, N - GATHER_V], BF16, name="k_tail", align_bytes=256)
         nc.vector.tensor_copy(out=k_dealt[:, 0:rows_v, :, PACK - 1], in_=last[:].indirect(offsets[:, 0:cols_v]))
         nc.scalar.activation(out=k_tail[:], in_=last[:].indirect(offsets[:, cols_v:]), func=COPY)
-        nc.vector.tensor_copy(
-            out=k_bf[:, :, rows_v:, PACK - 1], in_=k_tail[:].rearrange("p (s r) -> p r s", r=PACK)
-        )
+        tail_dealt = k_tail[:].rearrange("p (s r) -> p r s", r=PACK)
+        for tiles in (LOW, HIGH):
+            nc.vector.tensor_copy(out=k_bf[:, tiles, rows_v:, PACK - 1], in_=tail_dealt[:, tiles, :])
 
         q_scales = [keep.tile([P, QC], U8, name=f"q_scales{c}", align_bytes=256) for c in range(CHUNKS)]
         k_scales = [keep.tile([P, P], U8, name=f"k_scales{r}", align_bytes=256) for r in range(PACK)]
@@ -163,9 +163,10 @@ def tile_attend_plw_softf_f_topk_kernel(tc, qT, kT, ls, offs, out_0, out_1, out_
 
         for c in range(LAST):
             weave_q(nc.scalar.copy, c, q_raw[c][:], 3 + c)
+        k_words = [keep.tile([P, P], U32, name="k_words0", align_bytes=256)]
+        quantize(k_words[0][:], k_scales[0][:], k_bf[:, 0])
         quantize_q(0, 6, 2048)
-        k_words = []
-        for r in range(PACK):
+        for r in range(1, PACK):
             k_words.append(placed([P, P], U32, f"k_words{r}", 0, r * 512))
             quantize(k_words[r][:], k_scales[r][:], k_bf[:, r])
         scores(0)

@@ -105,7 +105,7 @@ def tile_attend_plw_softf_f_topk_kernel(tc, qT, kT, ls, offs, out_0, out_1, out_
         nc.vector.tensor_copy(out=k_dealt[:, 0:rows_v, :, PACK - 1], in_=last[:].indirect(offsets[:, 0:cols_v]))
         nc.scalar.activation(out=k_tail[:], in_=last[:].indirect(offsets[:, cols_v:]), func=COPY)
         tail_dealt = k_tail[:].rearrange("p (s r) -> p r s", r=PACK)
-        for tiles in (LOW, HIGH):
+        for tiles in (slice(0, 1), slice(1, PACK)):
             nc.vector.tensor_copy(out=k_bf[:, tiles, rows_v:, PACK - 1], in_=tail_dealt[:, tiles, :])
 
         q_scales = [keep.tile([P, QC], U8, name=f"q_scales{c}", align_bytes=256) for c in range(CHUNKS)]

from contextlib import ExitStack

import concourse.mybir as mybir
from concourse.masks import make_identity

D, T, N, NQ = 512, 2048, 512, 512
FLOPS = 2 * N * NQ * D

F32 = mybir.dt.float32
BF16 = mybir.dt.bfloat16
I32 = mybir.dt.int32
U32 = mybir.dt.uint32
U16 = mybir.dt.uint16
U8 = mybir.dt.uint8
FP8X4 = mybir.dt.float8_e4m3fn_x4
EXP = mybir.ActivationFunctionType.Exp
COPY = mybir.ActivationFunctionType.Copy
SUB = mybir.AluOpType.subtract
MULT = mybir.AluOpType.mult
ADD = mybir.AluOpType.add

P = 128
PACK = 4
LIST_ROWS = 16
QUADRANT = 32
QC = 128
CHUNKS = NQ // QC
LAST = CHUNKS - 1
HALF = NQ // 2
PAIR = 2
ROOM = 8192
LOW, HIGH, EVERY = slice(0, PAIR), slice(PAIR, PACK), slice(0, PACK)
UNITS = (tuple(slice(r, r + 1) for r in range(PACK)), (LOW, HIGH), (LOW, HIGH), (LOW, HIGH))
BANKS = 8
SHARE = 32
GATHER_V = 288
LS_ROW = 8
LS_ROWS = NQ // LS_ROW


def weave(copy, dst, src, run=PACK):
    copy(
        out=dst.rearrange("p (c i) t -> p c t i", i=run),
        in_=src.rearrange("p t (c i) -> p c t i", i=run),
    )


def tile_attend_plw_softf_f_topk_kernel(tc, qT, kT, ls, offs, out_0, out_1, out_2):
    nc = tc.nc

    def quantize(codes, scales, values):
        nc.vector.quantize_mx(out=codes.bitcast(FP8X4), scales=scales, in_=values.rearrange("p c t -> p (c t)"))

    def gpsimd_copy(out, in_):
        nc.gpsimd.tensor_scalar(out=out, in0=in_, scalar1=1.0, scalar2=0.0, op0=MULT, op1=ADD)

    def exp_to(out, in_):
        nc.scalar.activation(out=out, in_=in_, func=EXP)

    with ExitStack() as ctx:
        keep = ctx.enter_context(tc.tile_pool(name="keep", bufs=1))
        reuse = ctx.enter_context(tc.tile_pool(name="reuse", bufs=1))
        psum = ctx.enter_context(tc.psum_pool(name="psum", bufs=1))

        def placed(shape, dtype, name, room, byte=0):
            return reuse.tile(shape, dtype, name=name, offset=room * ROOM + byte, align_bytes=256)

        offsets = keep.tile([P, N // LIST_ROWS], U16, name="offsets")
        ls_col = keep.tile([P, LS_ROW], F32, name="ls_col")
        planes = [keep.tile([P, T], F32, name=f"plane{t}", align_bytes=256) for t in range(PACK)]
        q_raw = [placed([P, PACK, QC], F32, f"q_raw{c}", (0, 1, 16, 2)[c]) for c in range(CHUNKS)]
        k_rows = kT.rearrange("(p t) n -> t p n", t=PACK)
        q_rows = qT[0].rearrange("(p t) n -> p t n", t=PACK)
        nc.sync.dma_start(out=planes[0][:], in_=k_rows[0])
        nc.sync.dma_start(offsets[:], offs)
        nc.scalar.dma_start(out=ls_col[0:LS_ROWS, :], in_=ls[0, 0].rearrange("(p c) -> p c", c=LS_ROW))
        for t in range(1, PACK):
            nc.sync.dma_start(out=planes[t][:], in_=k_rows[t])
        for c in range(CHUNKS):
            nc.sync.dma_start(out=q_raw[c][:], in_=q_rows[:, :, c * QC : (c + 1) * QC])

        ident = keep.tile([P, P], F32, name="ident", align_bytes=256)
        make_identity(nc, ident[:])
        nc.gpsimd.memset(ls_col[LS_ROWS:, :], 0.0)
        ls_all = keep.tile([P, NQ], F32, name="ls_all", align_bytes=256)
        ls_out = ls_all[:].rearrange("p (n c) -> p n c", c=LS_ROW)
        for g in range(LS_ROW // PACK):
            ls_ps = psum.tile([P, PACK, P], F32, name=f"ls_ps{g}", tag=f"bank{BANKS - 1 - g}")
            for c in range(PACK):
                col = g * PACK + c
                nc.tensor.transpose(ls_ps[:, c, :], ls_col[:, col : col + 1].to_broadcast([P, P]), ident[:])
            nc.scalar.activation(
                out=ls_out[:, :, g * PACK : (g + 1) * PACK],
                in_=ls_ps[:, :, 0:LS_ROWS].rearrange("p c n -> p n c"),
                func=COPY,
            )

        k_bf = keep.tile([P, PACK, P, PACK], BF16, name="k_bf", align_bytes=256)
        k_dealt = k_bf[:].rearrange("p r s t -> p s r t")
        for t in range(PACK - 1):
            nc.vector.tensor_copy(out=k_dealt[:, :, :, t], in_=planes[t][:].indirect(offsets[:]))
        last = planes[PACK - 1]
        rows_v, cols_v = GATHER_V // PACK, GATHER_V // LIST_ROWS
        k_tail = keep.tile([P, N - GATHER_V], BF16, name="k_tail", align_bytes=256)
        nc.vector.tensor_copy(out=k_dealt[:, 0:rows_v, :, PACK - 1], in_=last[:].indirect(offsets[:, 0:cols_v]))
        nc.scalar.activation(out=k_tail[:], in_=last[:].indirect(offsets[:, cols_v:]), func=COPY)
        tail_dealt = k_tail[:].rearrange("p (s r) -> p r s", r=PACK)
        for tiles in (slice(0, 1), slice(1, PACK)):
            nc.vector.tensor_copy(out=k_bf[:, tiles, rows_v:, PACK - 1], in_=tail_dealt[:, tiles, :])

        q_scales = [keep.tile([P, QC], U8, name=f"q_scales{c}", align_bytes=256) for c in range(CHUNKS)]
        k_scales = [keep.tile([P, P], U8, name=f"k_scales{r}", align_bytes=256) for r in range(PACK)]
        y_rows = out_0.rearrange("(p r) q -> p r q", r=PACK)
        y = [keep.tile([P, PACK, HALF], F32, name=f"y{h}", align_bytes=256) for h in range(NQ // HALF)]
        q_bf, q_codes, banks = {}, {}, {}

        def weave_q(copy, c, src, room, byte=0):
            q_bf[c] = placed([P, QC, PACK], BF16, f"q_bf{c}", room, byte)
            weave(copy, q_bf[c][:], src, PAIR)

        def quantize_q(c, room, byte=0):
            q_codes[c] = placed([P, QC], U32, f"q_codes{c}", room, byte)
            quantize(q_codes[c][:], q_scales[c][:], q_bf[c][:])

        def scores(c):
            for tiles in UNITS[c]:
                u = (c, tiles.start)
                tag = f"bank{len(banks) % BANKS}"
                banks[u] = psum.tile([P, tiles.stop - tiles.start, QC], F32, name=f"scores{c}_{tiles.start}", tag=tag)
                for r in range(tiles.start, tiles.stop):
                    nc.tensor.matmul_mx(
                        out=banks[u][:, r - tiles.start, :],
                        lhsT=k_words[r][:].bitcast(FP8X4),
                        lhsT_scale=k_scales[r][:],
                        rhs=q_codes[c][:].bitcast(FP8X4),
                        rhs_scale=q_scales[c][:],
                        start=True,
                        stop=True,
                    )

        def y_part(c, tiles):
            h, lo = divmod(c * QC, HALF)
            return y[h][:, tiles, lo : lo + QC]

        shifted = {c: keep.tile([P, PACK, QC], F32, name=f"shifted{c}", align_bytes=256) for c in range(1, CHUNKS)}

        def weights(c, tiles, held=None, exp_tiles=None):
            u = (c, tiles.start)
            diff = shifted[c][:, tiles, :] if held is None else held[:]
            nc.vector.tensor_tensor(
                out=diff,
                in0=banks[u][:],
                in1=ls_all[:, c * QC : (c + 1) * QC].unsqueeze(1).to_broadcast([P, tiles.stop - tiles.start, QC]),
                op=SUB,
            )
            if exp_tiles is None:
                exp_to(y_part(c, tiles), diff)
            elif tiles.stop == exp_tiles.stop:
                exp_to(y_part(c, exp_tiles), shifted[c][:, exp_tiles, :])

        def store_unit(c, tiles):
            nc.sync.dma_start(out=y_rows[:, tiles, c * QC : (c + 1) * QC], in_=y_part(c, tiles))

        for c in range(LAST):
            weave_q(nc.scalar.copy, c, q_raw[c][:], 3 + c)
        k_words = [keep.tile([P, P], U32, name="k_words0", align_bytes=256)]
        quantize(k_words[0][:], k_scales[0][:], k_bf[:, 0])
        quantize_q(0, 6, 2048)
        for r in range(1, PACK):
            k_words.append(placed([P, P], U32, f"k_words{r}", 0, r * 512))
            quantize(k_words[r][:], k_scales[r][:], k_bf[:, r])
        scores(0)
        quantize_q(1, 7, 2048)
        scores(1)
        q_bf[LAST] = placed([P, QC, PACK], BF16, "q_bf3", 6, 2048 - 1024 + 256)
        weave(nc.scalar.copy, q_bf[LAST][:, SHARE:, :], q_raw[LAST][:, :, SHARE:], PAIR)
        shifted[0] = placed([P, PACK, QC], F32, "shifted0", 1)
        for tiles in UNITS[0]:
            weights(0, tiles, exp_tiles=LOW if tiles.start < PAIR else HIGH)
        store_unit(0, EVERY)
        quantize_q(2, 6, 2048 + 256)
        scores(2)
        weave(nc.vector.tensor_copy, q_bf[LAST][:, 0:SHARE, :], q_raw[LAST][:, :, 0:SHARE])
        weights(1, LOW)
        quantize_q(LAST, 7, 2048 + 256)
        scores(LAST)
        weights(1, HIGH, placed([P, PAIR, QC], F32, "held", 2))
        store_unit(1, EVERY)
        weights(2, LOW)
        weights(2, HIGH)
        for tiles in (LOW, HIGH):
            weights(LAST, tiles)
            nc.sync.dma_start(out=y_rows[:, tiles, HALF:], in_=y[1][:, tiles, :])

        y_codes = keep.tile([P, NQ], U32, name="y_codes", align_bytes=256)
        y_scales = keep.tile([P, NQ], U8, name="y_scales", align_bytes=256)
        y_bf0 = placed([P, QC, PACK], BF16, "y_bf0", 6, 512)
        y_bf1 = placed([P, QC, PACK], BF16, "y_bf1", 7, 2048 + 512)
        y_bf2 = placed([P, QC, PACK], BF16, "y_bf2", 14)
        y_bf3 = placed([P, QC, PACK], BF16, "y_bf3", 15)
        y_bf = [y_bf0, y_bf1, y_bf2, y_bf3]
        word_rows = out_1[0].rearrange("p q t -> p (q t)").bitcast(I32)

        def quantize_y(c):
            cols = slice(c * QC, (c + 1) * QC)
            quantize(y_codes[:, cols], y_scales[:, cols], y_bf[c][:])

        gpsimd_copy(y_bf0[:], y_part(0, EVERY).rearrange("p t c -> p c t"))
        weave(nc.vector.tensor_copy, y_bf1[:], y_part(1, EVERY))
        weave(nc.vector.tensor_copy, y_bf2[:], y_part(2, EVERY))
        split = 32
        weave(exp_to, y_bf3[:, split:, :], shifted[LAST][:, :, split:])
        quantize_y(0)
        quantize_y(1)
        nc.scalar.dma_start(out=word_rows[:, 0:HALF], in_=y_codes[:, 0:HALF].bitcast(I32))
        weave(nc.vector.tensor_copy, y_bf3[:, 0:split, :], y[1][:, :, QC : QC + split])
        quantize_y(2)
        quantize_y(LAST)
        nc.sync.dma_start(out=word_rows[:, HALF:], in_=y_codes[:, HALF:].bitcast(I32))

        scale_rows = out_2[0].bitcast(I32)
        for quad in range(P // QUADRANT):
            nc.scalar.dma_start(
                out=scale_rows[PACK * quad : PACK * (quad + 1), :],
                in_=y_scales[QUADRANT * quad : QUADRANT * quad + PACK, :].bitcast(I32),
            )
